import numpy as np
import ml_dtypes


def mxq(x, axis, fmt="e4m3"):
    dtype, down = {"e4m3": (ml_dtypes.float8_e4m3fn, 7), "e5m2": (ml_dtypes.float8_e5m2, 14)}[fmt]
    v = np.moveaxis(np.asarray(x, np.float32).astype(ml_dtypes.bfloat16).astype(np.float64), axis, -1)
    blocks = v.reshape(v.shape[:-1] + (-1, 32))
    amax = np.abs(blocks).max(-1, keepdims=True)
    byte = np.maximum(np.where(amax > 0, np.frexp(amax)[1] - 1 + 127, 0) - down, 1)
    scale = np.exp2(byte - 127.0)
    codes = (blocks / scale).astype(np.float32).astype(dtype).astype(np.float64)
    return np.moveaxis((codes * scale).reshape(v.shape), -1, axis)


WIDE = False


def mx_kscale(k):
    if not WIDE:
        return np.ones(k)
    levels = np.array([10, -10, 5, -5, 0])
    if k % 512:
        return np.exp2(np.random.permutation(np.resize(levels, k // 32))).repeat(32)
    a = np.empty((k // 512, 16))
    for p in range(k // 512):
        a[p, :8] = np.random.permutation(np.resize(levels, 8))
        for g in range(8):
            far = levels[np.abs(levels - a[p, g]) >= 10]
            a[p, g + 8] = far[np.random.randint(len(far))]
    return np.exp2(a.ravel()).repeat(32)


def f64(x):
    return np.asarray(x).astype(np.float64)


def striped(idx):
    return np.tile(idx.reshape(-1, 16).T, (8, 1)).astype(np.uint16)


def unstriped(offs):
    return offs[:16].T.reshape(-1).astype(np.int64)


E2M1 = np.array([0.0, 0.5, 1.0, 1.5, 2.0, 3.0, 4.0, 6.0, -0.0, -0.5, -1.0, -1.5, -2.0, -3.0, -4.0, -6.0])


def pack_weight(w, fmt):
    k, n = w.shape
    w = f64(np.asarray(w, np.float32).astype(ml_dtypes.bfloat16)).reshape(k // 32, 32, n)
    amax = np.abs(w).max(1)
    if fmt == "e4m3":
        byte = np.frexp(amax)[1] - 1 + 127 - 7
    else:
        mant, ex = np.frexp(amax / 6.0)
        byte = np.where(mant > 0.5, ex, ex - 1) + 127
    byte = np.clip(np.where(amax > 0, byte, 1), 1, 254)
    scaled = (w * np.exp2(127.0 - byte)[:, None, :]).reshape(k, n).astype(np.float32)
    by_word = np.ascontiguousarray(scaled.reshape(k // 512, 128, 4, n).transpose(0, 1, 3, 2))
    if fmt == "e4m3":
        words = by_word.astype(ml_dtypes.float8_e4m3fn).view(np.uint8)
    else:
        c = by_word.astype(ml_dtypes.float4_e2m1fn).view(np.uint8) & 0xF
        words = (c[..., 0::2] | (c[..., 1::2] << 4)).reshape(k // 512, 128, 2 * n)
    return np.ascontiguousarray(words), np.ascontiguousarray(byte.astype(np.uint8).reshape(k // 512, 16, n))


def unpack_weight(words, scales, fmt):
    g, _, n = scales.shape
    words = np.ascontiguousarray(words).reshape(g, 128, n, -1)
    if fmt == "e4m3":
        vals = words.view(ml_dtypes.float8_e4m3fn).astype(np.float64)
    else:
        nib = np.empty((g, 128, n, 4), np.uint8)
        nib[..., 0::2] = words & 0xF
        nib[..., 1::2] = words >> 4
        vals = E2M1[nib]
    vals = vals * np.repeat(np.exp2(scales.astype(np.float64) - 127.0), 8, axis=1)[..., None]
    return vals.transpose(0, 1, 3, 2).reshape(g * 512, n)


def planes(y):
    n, m = y.shape
    v = y.astype(np.float32).astype(ml_dtypes.bfloat16).astype(np.float64).reshape(n // 32, 32, m)
    top = np.abs(v).max(1)
    byte = np.clip(np.where(top > 0, np.frexp(top)[1] - 1 + 127 - 7, 1), 1, 254)
    codes = (v * np.exp2(127.0 - byte)[:, None, :]).reshape(n, m).astype(np.float32).astype(ml_dtypes.float8_e4m3fn).view(np.uint8)
    words = codes.reshape(n // 512, 128, 4, m).transpose(0, 1, 3, 2)
    return np.ascontiguousarray(words), np.ascontiguousarray(byte.astype(np.uint8).reshape(n // 512, 16, m))


def silu(v):
    return v / (1.0 + np.exp(-np.maximum(v, -700.0)))


K, T, E, G, H, N = 512, 512, 6, 2, 512, 512


def setup_inputs():
    n = np.random.standard_normal
    s = mx_kscale(K)
    u = mx_kscale(H)
    chosen = np.random.permutation(E)[:G]
    x = pack_weight(n((K, T)) * s[:, None], "e4m3")
    w1 = pack_weight(n((K, E * H)) / np.sqrt(K) / s[:, None] * np.tile(u, E), "e4m3")
    w2 = pack_weight(n((H, E * N)) / np.sqrt(H) / u[:, None], "e4m3")
    return {
        "x_words": x[0],
        "x_scales": x[1],
        "w1_words": w1[0],
        "w1_scales": w1[1],
        "w2_words": w2[0],
        "w2_scales": w2[1],
        "gate": np.stack([np.tile(r, (128, 1)) for r in np.random.uniform(0.2, 1.0, (G, T))]).astype(np.float32),
        "offs": striped((chosen[:, None] * H + np.arange(H)).reshape(-1)),
        "offs2": striped((chosen[:, None] * N + np.arange(N)).reshape(-1)),
    }


def reference(x_words, x_scales, w1_words, w1_scales, w2_words, w2_scales, gate, offs, offs2):
    idx, idx2 = unstriped(offs), unstriped(offs2)
    x = unpack_weight(x_words, x_scales, "e4m3")
    w1 = unpack_weight(w1_words, w1_scales, "e4m3")[:, idx]
    w2 = unpack_weight(w2_words, w2_scales, "e4m3")[:, idx2]
    y = np.zeros((N, T))
    for r in range(G):
        h = f64(gate[r, :1]) * silu(w1[:, r * H:(r + 1) * H].T @ x)
        y = y + w2[:, r * N:(r + 1) * N].T @ mxq(h, 0, "e4m3")
    out_0 = y
    return (out_0,) + planes(out_0)

@@ -1,0 +1,210 @@
+from contextlib import ExitStack
+
+import concourse.mybir as mybir
+
+K, T, E, G, H, N = 512, 512, 6, 2, 512, 512
+FLOPS = 2 * G * T * (K * H + H * N)
+
+F32 = mybir.dt.float32
+BF16 = mybir.dt.bfloat16
+I32 = mybir.dt.int32
+U32 = mybir.dt.uint32
+U16 = mybir.dt.uint16
+U8 = mybir.dt.uint8
+FP8X4 = mybir.dt.float8_e4m3fn_x4
+SILU = mybir.ActivationFunctionType.Silu
+MULT = mybir.AluOpType.mult
+
+P = 128
+PACK = 4
+CHUNKS = T // P
+LIST_COLS = H // 16
+X_ROW = 8
+W2_ROW = 4
+
+
+def load_scale_rows(queue, plane, scales, first_row):
+    for q in range(4):
+        row = 32 * q + first_row
+        queue.dma_start(out=plane[row:row + 4, :].bitcast(I32), in_=scales[0, 4 * q:4 * q + 4, :].bitcast(I32))
+
+
+def words_of(packed):
+    return packed[0].rearrange("p m d -> p (m d)").bitcast(I32)
+
+
+def tile_moe_wsel_b_silu_p_kernel(
+    tc, x_words, x_scales, w1_words, w1_scales, w2_words, w2_scales, gate, offs, offs2, out_0, out_1, out_2
+):
+    nc = tc.nc
+    with ExitStack() as ctx:
+        keep = ctx.enter_context(tc.tile_pool(name="keep", bufs=1))
+        ring = ctx.enter_context(tc.tile_pool(name="ring", bufs=8))
+        psum = ctx.enter_context(tc.psum_pool(name="psum", bufs=1))
+
+        list1 = keep.tile([P, G * LIST_COLS], U16)
+        list2 = keep.tile([P, G * LIST_COLS], U16)
+        w1s_all = keep.tile([P, E * H], U8, align_bytes=64)
+        w2s_all = keep.tile([P, E * N], U8, align_bytes=64)
+        x_codes = keep.tile([P, T], I32, align_bytes=64)
+        x_plane = keep.tile([P, T], U8, align_bytes=64)
+        zeros = keep.tile([P, P], F32, align_bytes=64, tag="first_matrices")
+        gate_rows = keep.tile([P, P], F32, align_bytes=64, tag="second_matrices")
+        ident = keep.tile([P, P], F32)
+
+        nc.gpsimd.memset(w1s_all[:].bitcast(I32), 0)
+        nc.gpsimd.memset(zeros[:], 0.0)
+        nc.gpsimd.affine_select(
+            out=ident[:],
+            in_=zeros[:],
+            compare_op=mybir.AluOpType.not_equal,
+            fill=1.0,
+            base=0,
+            pattern=[[-1, P]],
+            channel_multiplier=1,
+        )
+        nc.gpsimd.memset(gate_rows[:], 0.0)
+        nc.gpsimd.memset(x_plane[:].bitcast(I32), 0)
+        nc.gpsimd.memset(w2s_all[:].bitcast(I32), 0)
+
+        nc.sync.dma_start(list1[:], offs)
+        nc.sync.dma_start(list2[:], offs2)
+        nc.sync.dma_start(out=x_codes[:], in_=words_of(x_words))
+        load_scale_rows(nc.sync, w1s_all, w1_scales, 0)
+        w1_all = keep.tile([P, E * H], I32, align_bytes=64, tag="first_matrices")
+        nc.sync.dma_start(out=w1_all[:], in_=words_of(w1_words))
+        gate_runs = gate.rearrange("r q (c p) -> (r q c) p", p=P)
+        nc.scalar.dma_start(out=gate_rows[0:G * CHUNKS, :], in_=gate_runs[0:G * P * CHUNKS:P + 1, :])
+        load_scale_rows(nc.scalar, x_plane, x_scales, X_ROW)
+        load_scale_rows(nc.sync, w2s_all, w2_scales, W2_ROW)
+
+        gate_bank = psum.tile([P, P], F32, tag="bank7")
+        nc.tensor.transpose(gate_bank[:], gate_rows[:], ident[:])
+        w2_all = keep.tile([P, E * N], I32, align_bytes=64, tag="second_matrices")
+        nc.scalar.dma_start(out=w2_all[:], in_=words_of(w2_words))
+        gate_cols = keep.tile([P, G * CHUNKS], F32)
+        nc.vector.tensor_copy(out=gate_cols[:], in_=gate_bank[:, 0:G * CHUNKS])
+
+        w1_codes, w1_planes = [], []
+        for r in range(G):
+            picked_plane = keep.tile([P, H], U8, align_bytes=64, name="w1_plane%d" % r)
+            nc.vector.tensor_copy(
+                out=picked_plane[:], in_=w1s_all[:].indirect(list1[:, r * LIST_COLS:(r + 1) * LIST_COLS])
+            )
+            w1_planes.append(picked_plane)
+            picked = keep.tile([P, H], I32, align_bytes=64, name="w1_codes%d" % r)
+            nc.vector.tensor_copy(
+                out=picked[:].bitcast(U32),
+                in_=w1_all[:].bitcast(U32).indirect(list1[:, r * LIST_COLS:(r + 1) * LIST_COLS]),
+            )
+            w1_codes.append(picked)
+
+        w2_codes = []
+        for r in range(G):
+            picked2 = keep.tile([P, N], I32, align_bytes=64, name="w2_picked%d" % r)
+            nc.vector.tensor_copy(
+                out=picked2[:].bitcast(U32),
+                in_=w2_all[:].bitcast(U32).indirect(list2[:, r * LIST_COLS:(r + 1) * LIST_COLS]),
+            )
+            dealt = keep.tile([P, N], I32, align_bytes=64, name="w2_codes%d" % r)
+            nc.vector.tensor_copy(
+                out=dealt[:].rearrange("p (j b i) -> p b j i", j=PACK, i=4),
+                in_=picked2[:].rearrange("p (b i j) -> p b j i", j=PACK, i=4),
+            )
+            w2_codes.append(dealt)
+        w2s_picked = keep.tile([P, G * N], U8, align_bytes=64)
+        nc.vector.tensor_copy(out=w2s_picked[:], in_=w2s_all[:].indirect(list2[:]))
+        w2_plane = keep.tile([P, G * N], U8, align_bytes=64)
+        nc.vector.tensor_copy(
+            out=w2_plane[:].rearrange("p (r j b i) -> p r b j i", r=G, j=PACK, i=16),
+            in_=w2s_picked[:].rearrange("p (r b i j) -> p r b j i", r=G, j=PACK, i=16),
+        )
+
+        y_codes = keep.tile([P, T], I32, align_bytes=64)
+        y_plane = keep.tile([P, T], U8, align_bytes=64)
+        out_rows = out_0.rearrange("(p j) t -> p j t", j=PACK)
+        out_words = words_of(out_1)
+
+        units = [(half, r, cc) for half in range(2) for r in range(G) for cc in range(2)]
+        acts = {}
+        for k, (half, r, cc) in enumerate(units):
+            c = 2 * half + cc
+            tokens = slice(c * P, (c + 1) * P)
+            pre = psum.tile([P, H], F32, tag="bank%d" % (k % 6))
+            nc.tensor.matmul_mx(
+                out=pre[:],
+                lhsT=x_codes[:, tokens].bitcast(FP8X4),
+                lhsT_scale=x_plane[X_ROW:P, tokens],
+                rhs=w1_codes[r][:].bitcast(FP8X4),
+                rhs_scale=w1_planes[r][:],
+                start=True,
+                stop=True,
+            )
+            act = ring.tile([P, H], F32)
+            nc.scalar.activation(
+                out=act[:].rearrange("p (u m e) -> p u m e", u=2, e=2),
+                in_=pre[:].rearrange("p (m u e) -> p u m e", u=2, e=2),
+                func=SILU,
+            )
+            acts[r, c] = act
+
+        for half in range(2):
+            h_codes, h_planes = [], []
+            for r in range(G):
+                turned = psum.tile([P, 2, 2, P], F32, tag="bank%d" % r)
+                for cc in range(2):
+                    c = 2 * half + cc
+                    h_tok = ring.tile([P, H], BF16)
+                    col = r * CHUNKS + c
+                    nc.vector.tensor_scalar(
+                        out=h_tok[:], in0=acts[r, c][:], scalar1=gate_cols[:, col:col + 1], scalar2=None, op0=MULT
+                    )
+                    pairs = h_tok[:].bitcast(F32)
+                    for u in range(2):
+                        nc.tensor.transpose(turned[:, cc, u, :], pairs[:, u * P:(u + 1) * P], ident[:])
+                h_grouped = ring.tile([P, 2 * P * PACK], BF16, align_bytes=64)
+                nc.scalar.copy(
+                    out=h_grouped[:].bitcast(F32).rearrange("p (c t u) -> p c t u", c=2, u=2),
+                    in_=turned[:].rearrange("p c u t -> p c t u"),
+                )
+                codes = ring.tile([P, 2 * P], I32, align_bytes=64)
+                plane = ring.tile([P, 2 * P], U8, align_bytes=64)
+                nc.vector.quantize_mx(out=codes[:].bitcast(FP8X4), scales=plane[:], in_=h_grouped[:])
+                h_codes.append(codes)
+                h_planes.append(plane)
+
+            for cc in range(2):
+                c = 2 * half + cc
+                tokens = slice(c * P, (c + 1) * P)
+                local = slice(cc * P, (cc + 1) * P)
+                acc = psum.tile([P, PACK, P], F32, tag="bank%d" % (2 + c))
+                for j in range(PACK):
+                    for r in range(G):
+                        nc.tensor.matmul_mx(
+                            out=acc[:, j, :],
+                            lhsT=w2_codes[r][:, j * P:(j + 1) * P].bitcast(FP8X4),
+                            lhsT_scale=w2_plane[W2_ROW:P, r * N + j * P:r * N + (j + 1) * P],
+                            rhs=h_codes[r][:, local].bitcast(FP8X4),
+                            rhs_scale=h_planes[r][:, local],
+                            start=(r == 0),
+                            stop=(r == G - 1),
+                        )
+                y = ring.tile([P, PACK * P], F32)
+                nc.scalar.copy(out=y[:], in_=acc[:].rearrange("p j t -> p (j t)"))
+                nc.sync.dma_start(out=out_rows[:, :, tokens], in_=y[:].rearrange("p (j t) -> p j t", j=PACK))
+                y_grouped = ring.tile([P, P * PACK], BF16, align_bytes=64)
+                nc.vector.tensor_copy(
+                    out=y_grouped[:].rearrange("p (b i j) -> p b j i", j=PACK, i=4),
+                    in_=y[:].rearrange("p (j b i) -> p b j i", j=PACK, i=4),
+                )
+                nc.vector.quantize_mx(
+                    out=y_codes[:, tokens].bitcast(FP8X4), scales=y_plane[:, tokens], in_=y_grouped[:]
+                )
+            both = slice(half * 2 * P, (half + 1) * 2 * P)
+            nc.sync.dma_start(out=out_words[:, both], in_=y_codes[:, both])
+
+        for q in range(4):
+            queue = nc.scalar if q % 2 else nc.sync
+            queue.dma_start(
+                out=out_2[0, 4 * q:4 * q + 4, :].bitcast(I32), in_=y_plane[32 * q:32 * q + 4, :].bitcast(I32)
+            )

@@ -13,6 +13,7 @@ U16 = mybir.dt.uint16
 U8 = mybir.dt.uint8
 FP8X4 = mybir.dt.float8_e4m3fn_x4
 SILU = mybir.ActivationFunctionType.Silu
+COPY = mybir.ActivationFunctionType.Copy
 MULT = mybir.AluOpType.mult
 
 P = 128
@@ -23,10 +24,10 @@ X_ROW = 8
 W2_ROW = 4
 
 
-def load_scale_rows(queue, plane, scales, first_row):
+def load_scale_rows(queues, plane, scales, first_row):
     for q in range(4):
         row = 32 * q + first_row
-        queue.dma_start(out=plane[row:row + 4, :].bitcast(I32), in_=scales[0, 4 * q:4 * q + 4, :].bitcast(I32))
+        queues[q % len(queues)].dma_start(out=plane[row:row + 4, :].bitcast(I32), in_=scales[0, 4 * q:4 * q + 4, :].bitcast(I32))
 
 
 def words_of(packed):
@@ -52,7 +53,8 @@ def tile_moe_wsel_b_silu_p_kernel(
         gate_rows = keep.tile([P, P], F32, align_bytes=64, tag="second_matrices")
         ident = keep.tile([P, P], F32)
 
-        nc.gpsimd.memset(w1s_all[:].bitcast(I32), 0)
+        nc.gpsimd.memset(w1s_all[:, 0:E * H // 2].bitcast(I32), 0)
+        nc.vector.memset(w1s_all[:, E * H // 2:E * H].bitcast(I32), 0)
         nc.gpsimd.memset(zeros[:], 0.0)
         nc.gpsimd.affine_select(
             out=ident[:],
@@ -63,25 +65,26 @@ def tile_moe_wsel_b_silu_p_kernel(
             pattern=[[-1, P]],
             channel_multiplier=1,
         )
+        nc.gpsimd.memset(w2s_all[:, 0:E * N // 2].bitcast(I32), 0)
         nc.gpsimd.memset(gate_rows[:], 0.0)
         nc.gpsimd.memset(x_plane[:].bitcast(I32), 0)
-        nc.gpsimd.memset(w2s_all[:].bitcast(I32), 0)
+        nc.gpsimd.memset(w2s_all[:, E * N // 2:E * N].bitcast(I32), 0)
 
         nc.sync.dma_start(list1[:], offs)
         nc.sync.dma_start(list2[:], offs2)
         nc.sync.dma_start(out=x_codes[:], in_=words_of(x_words))
-        load_scale_rows(nc.sync, w1s_all, w1_scales, 0)
+        load_scale_rows([nc.sync, nc.scalar], w1s_all, w1_scales, 0)
         w1_all = keep.tile([P, E * H], I32, align_bytes=64, tag="first_matrices")
         nc.sync.dma_start(out=w1_all[:], in_=words_of(w1_words))
         gate_runs = gate.rearrange("r q (c p) -> (r q c) p", p=P)
         nc.scalar.dma_start(out=gate_rows[0:G * CHUNKS, :], in_=gate_runs[0:G * P * CHUNKS:P + 1, :])
-        load_scale_rows(nc.scalar, x_plane, x_scales, X_ROW)
-        load_scale_rows(nc.sync, w2s_all, w2_scales, W2_ROW)
+        load_scale_rows([nc.scalar], x_plane, x_scales, X_ROW)
+        load_scale_rows([nc.sync], w2s_all, w2_scales, W2_ROW)
 
         gate_bank = psum.tile([P, P], F32, tag="bank7")
         nc.tensor.transpose(gate_bank[:], gate_rows[:], ident[:])
         w2_all = keep.tile([P, E * N], I32, align_bytes=64, tag="second_matrices")
-        nc.scalar.dma_start(out=w2_all[:], in_=words_of(w2_words))
+        nc.sync.dma_start(out=w2_all[:], in_=words_of(w2_words))
         gate_cols = keep.tile([P, G * CHUNKS], F32)
         nc.vector.tensor_copy(out=gate_cols[:], in_=gate_bank[:, 0:G * CHUNKS])
 
@@ -92,6 +95,7 @@ def tile_moe_wsel_b_silu_p_kernel(
                 out=picked_plane[:], in_=w1s_all[:].indirect(list1[:, r * LIST_COLS:(r + 1) * LIST_COLS])
             )
             w1_planes.append(picked_plane)
+        for r in range(G):
             picked = keep.tile([P, H], I32, align_bytes=64, name="w1_codes%d" % r)
             nc.vector.tensor_copy(
                 out=picked[:].bitcast(U32),
@@ -99,20 +103,7 @@ def tile_moe_wsel_b_silu_p_kernel(
             )
             w1_codes.append(picked)
 
-        w2_codes = []
-        for r in range(G):
-            picked2 = keep.tile([P, N], I32, align_bytes=64, name="w2_picked%d" % r)
-            nc.vector.tensor_copy(
-                out=picked2[:].bitcast(U32),
-                in_=w2_all[:].bitcast(U32).indirect(list2[:, r * LIST_COLS:(r + 1) * LIST_COLS]),
-            )
-            dealt = keep.tile([P, N], I32, align_bytes=64, name="w2_codes%d" % r)
-            nc.vector.tensor_copy(
-                out=dealt[:].rearrange("p (j b i) -> p b j i", j=PACK, i=4),
-                in_=picked2[:].rearrange("p (b i j) -> p b j i", j=PACK, i=4),
-            )
-            w2_codes.append(dealt)
-        w2s_picked = keep.tile([P, G * N], U8, align_bytes=64)
+        w2s_picked = keep.tile([P, G * N], U8, align_bytes=64, tag="first_matrices")
         nc.vector.tensor_copy(out=w2s_picked[:], in_=w2s_all[:].indirect(list2[:]))
         w2_plane = keep.tile([P, G * N], U8, align_bytes=64)
         nc.vector.tensor_copy(
@@ -140,7 +131,7 @@ def tile_moe_wsel_b_silu_p_kernel(
                 start=True,
                 stop=True,
             )
-            act = ring.tile([P, H], F32)
+            act = keep.tile([P, H], F32, align_bytes=64, tag="act%d" % k)
             nc.scalar.activation(
                 out=act[:].rearrange("p (u m e) -> p u m e", u=2, e=2),
                 in_=pre[:].rearrange("p (m u e) -> p u m e", u=2, e=2),
@@ -148,31 +139,65 @@ def tile_moe_wsel_b_silu_p_kernel(
             )
             acts[r, c] = act
 
-        for half in range(2):
-            h_codes, h_planes = [], []
-            for r in range(G):
-                turned = psum.tile([P, 2, 2, P], F32, tag="bank%d" % r)
-                for cc in range(2):
-                    c = 2 * half + cc
-                    h_tok = ring.tile([P, H], BF16)
-                    col = r * CHUNKS + c
+        def apply_gate(half, r):
+            gated = []
+            for cc in range(2):
+                c = 2 * half + cc
+                col = r * CHUNKS + c
+                tag = "first_matrices" if (r, c) == (0, 0) else "gated%d" % col
+                h_tok = keep.tile([P, H], BF16, align_bytes=64, tag=tag)
+                if half == 0:
                     nc.vector.tensor_scalar(
                         out=h_tok[:], in0=acts[r, c][:], scalar1=gate_cols[:, col:col + 1], scalar2=None, op0=MULT
                     )
-                    pairs = h_tok[:].bitcast(F32)
-                    for u in range(2):
-                        nc.tensor.transpose(turned[:, cc, u, :], pairs[:, u * P:(u + 1) * P], ident[:])
-                h_grouped = ring.tile([P, 2 * P * PACK], BF16, align_bytes=64)
-                nc.scalar.copy(
-                    out=h_grouped[:].bitcast(F32).rearrange("p (c t u) -> p c t u", c=2, u=2),
-                    in_=turned[:].rearrange("p c u t -> p c t u"),
-                )
-                codes = ring.tile([P, 2 * P], I32, align_bytes=64)
-                plane = ring.tile([P, 2 * P], U8, align_bytes=64)
-                nc.vector.quantize_mx(out=codes[:].bitcast(FP8X4), scales=plane[:], in_=h_grouped[:])
-                h_codes.append(codes)
-                h_planes.append(plane)
+                else:
+                    nc.scalar.activation(out=h_tok[:], in_=acts[r, c][:], func=COPY, scale=gate_cols[:, col:col + 1])
+                gated.append(h_tok)
+            return gated
 
+        def turn_and_quantize(r, gated):
+            turned = psum.tile([P, 2, 2, P], F32, tag="bank%d" % r)
+            for cc in range(2):
+                pairs = gated[cc][:].bitcast(F32)
+                for u in range(2):
+                    nc.tensor.transpose(turned[:, cc, u, :], pairs[:, u * P:(u + 1) * P], ident[:])
+            h_grouped = ring.tile([P, 2 * P * PACK], BF16, align_bytes=64)
+            nc.scalar.copy(
+                out=h_grouped[:].bitcast(F32).rearrange("p (c t u) -> p c t u", c=2, u=2),
+                in_=turned[:].rearrange("p c u t -> p c t u"),
+            )
+            codes = ring.tile([P, 2 * P], I32, align_bytes=64)
+            plane = ring.tile([P, 2 * P], U8, align_bytes=64)
+            nc.vector.quantize_mx(out=codes[:].bitcast(FP8X4), scales=plane[:], in_=h_grouped[:])
+            return codes, plane
+
+        gated = {(0, r): apply_gate(0, r) for r in range(G)}
+        w2_picked = keep.tile([P, G * N], I32, align_bytes=64, tag="act3")
+        for r in range(G):
+            nc.vector.tensor_copy(
+                out=w2_picked[:, r * N:(r + 1) * N].bitcast(U32),
+                in_=w2_all[:].bitcast(U32).indirect(list2[:, r * LIST_COLS:(r + 1) * LIST_COLS]),
+            )
+
+        def deal(r, tag):
+            dealt = keep.tile([P, N], I32, align_bytes=64, tag=tag)
+            nc.vector.tensor_copy(
+                out=dealt[:].rearrange("p (j b i) -> p b j i", j=PACK, i=4),
+                in_=w2_picked[:, r * N:(r + 1) * N].rearrange("p (b i j) -> p b j i", j=PACK, i=4),
+            )
+            return dealt
+
+        w2_codes = [deal(0, "w2_codes0")]
+        gated[1, 0] = apply_gate(1, 0)
+        hq = {(0, r): turn_and_quantize(r, gated[0, r]) for r in range(G)}
+        gated[1, 1] = apply_gate(1, 1)
+        w2_codes.append(deal(1, "act7"))
+        for r in range(G):
+            hq[1, r] = turn_and_quantize(r, gated[1, r])
+
+        for half in range(2):
+            h_codes = [hq[half, r][0] for r in range(G)]
+            h_planes = [hq[half, r][1] for r in range(G)]
             for cc in range(2):
                 c = 2 * half + cc
                 tokens = slice(c * P, (c + 1) * P)
@@ -200,8 +225,7 @@ def tile_moe_wsel_b_silu_p_kernel(
                 nc.vector.quantize_mx(
                     out=y_codes[:, tokens].bitcast(FP8X4), scales=y_plane[:, tokens], in_=y_grouped[:]
                 )
-            both = slice(half * 2 * P, (half + 1) * 2 * P)
-            nc.sync.dma_start(out=out_words[:, both], in_=y_codes[:, both])
+                nc.sync.dma_start(out=out_words[:, tokens], in_=y_codes[:, tokens])
 
         for q in range(4):
             queue = nc.scalar if q % 2 else nc.sync

@@ -15,19 +15,23 @@ FP8X4 = mybir.dt.float8_e4m3fn_x4
 SILU = mybir.ActivationFunctionType.Silu
 COPY = mybir.ActivationFunctionType.Copy
 MULT = mybir.AluOpType.mult
+ADD = mybir.AluOpType.add
 
 P = 128
 PACK = 4
 CHUNKS = T // P
 LIST_COLS = H // 16
 X_ROW = 8
+EARLY = 1024
+GATE_ENGINE = "vvvvvvss"
 W2_ROW = 4
 
 
 def load_scale_rows(queues, plane, scales, first_row):
     for q in range(4):
-        row = 32 * q + first_row
-        queues[q % len(queues)].dma_start(out=plane[row:row + 4, :].bitcast(I32), in_=scales[0, 4 * q:4 * q + 4, :].bitcast(I32))
+        queues[q % len(queues)].dma_start(
+            out=plane[first_row + q:P:32, :].bitcast(I32), in_=scales[0, q:16:4, :].bitcast(I32)
+        )
 
 
 def words_of(packed):
@@ -45,71 +49,61 @@ def tile_moe_wsel_b_silu_p_kernel(
 
         list1 = keep.tile([P, G * LIST_COLS], U16)
         list2 = keep.tile([P, G * LIST_COLS], U16)
-        w1s_all = keep.tile([P, E * H], U8, align_bytes=64)
-        w2s_all = keep.tile([P, E * N], U8, align_bytes=64)
-        x_codes = keep.tile([P, T], I32, align_bytes=64)
+        w1s_all = keep.tile([P, E * H], U8, align_bytes=64, tag="first_scales")
+        w2s_all = keep.tile([P, E * N], U8, align_bytes=64, tag="second_scales")
         x_plane = keep.tile([P, T], U8, align_bytes=64)
-        zeros = keep.tile([P, P], F32, align_bytes=64, tag="first_matrices")
+        w1_all = keep.tile([P, E * H], I32, align_bytes=64, tag="first_matrices")
+        zeros2 = keep.tile([P, P], F32, align_bytes=64, tag="tokens")
         gate_rows = keep.tile([P, P], F32, align_bytes=64, tag="second_matrices")
         ident = keep.tile([P, P], F32)
 
         nc.gpsimd.memset(w1s_all[:, 0:E * H // 2].bitcast(I32), 0)
-        nc.vector.memset(w1s_all[:, E * H // 2:E * H].bitcast(I32), 0)
-        nc.gpsimd.memset(zeros[:], 0.0)
+        nc.gpsimd.memset(w1_all[:, EARLY:EARLY + P], 0)
+        nc.gpsimd.memset(zeros2[:], 0.0)
+        nc.gpsimd.memset(gate_rows[:], 0.0)
+        gate_runs = gate.rearrange("r q (c p) -> (r q c) p", p=P)
         nc.gpsimd.affine_select(
             out=ident[:],
-            in_=zeros[:],
+            in_=zeros2[:],
             compare_op=mybir.AluOpType.not_equal,
             fill=1.0,
             base=0,
             pattern=[[-1, P]],
             channel_multiplier=1,
         )
-        nc.gpsimd.memset(w2s_all[:, 0:E * N // 2].bitcast(I32), 0)
-        nc.gpsimd.memset(gate_rows[:], 0.0)
-        nc.gpsimd.memset(x_plane[:].bitcast(I32), 0)
-        nc.gpsimd.memset(w2s_all[:, E * N // 2:E * N].bitcast(I32), 0)
+        no_bias = keep.tile([P, 1], F32, align_bytes=64, tag="gate_cols")
+        zero_col = keep.tile([P, 1], F32, align_bytes=64)
+        nc.gpsimd.memset(zero_col[:], 0.0)
+        nc.scalar.activation(out=no_bias[:], in_=zero_col[:], func=SILU)
+        nc.vector.memset(w1s_all[:, E * H // 2:E * H].bitcast(I32), 0)
+        nc.vector.tensor_copy(out=x_plane[:].bitcast(I32), in_=w1_all[:, EARLY:EARLY + P])
+        nc.vector.memset(w2s_all[:].bitcast(I32), 0)
 
         nc.sync.dma_start(list1[:], offs)
         nc.sync.dma_start(list2[:], offs2)
+        nc.sync.dma_start(out=w1_all[:, 0:EARLY], in_=words_of(w1_words)[:, 0:EARLY])
+        load_scale_rows([nc.sync], w1s_all, w1_scales, 0)
+        nc.sync.dma_start(out=w1_all[:, EARLY:E * H], in_=words_of(w1_words)[:, EARLY:E * H])
+        nc.sync.dma_start(out=gate_rows[0:G * CHUNKS, :], in_=gate_runs[0:G * P * CHUNKS:P + 1, :])
+        x_codes = keep.tile([P, T], I32, align_bytes=64, tag="tokens")
         nc.sync.dma_start(out=x_codes[:], in_=words_of(x_words))
-        load_scale_rows([nc.sync, nc.scalar], w1s_all, w1_scales, 0)
-        w1_all = keep.tile([P, E * H], I32, align_bytes=64, tag="first_matrices")
-        nc.sync.dma_start(out=w1_all[:], in_=words_of(w1_words))
-        gate_runs = gate.rearrange("r q (c p) -> (r q c) p", p=P)
-        nc.scalar.dma_start(out=gate_rows[0:G * CHUNKS, :], in_=gate_runs[0:G * P * CHUNKS:P + 1, :])
-        load_scale_rows([nc.scalar], x_plane, x_scales, X_ROW)
+        load_scale_rows([nc.sync], x_plane, x_scales, X_ROW)
         load_scale_rows([nc.sync], w2s_all, w2_scales, W2_ROW)
-
         gate_bank = psum.tile([P, P], F32, tag="bank7")
         nc.tensor.transpose(gate_bank[:], gate_rows[:], ident[:])
         w2_all = keep.tile([P, E * N], I32, align_bytes=64, tag="second_matrices")
         nc.sync.dma_start(out=w2_all[:], in_=words_of(w2_words))
-        gate_cols = keep.tile([P, G * CHUNKS], F32)
-        nc.vector.tensor_copy(out=gate_cols[:], in_=gate_bank[:, 0:G * CHUNKS])
 
-        w1_codes, w1_planes = [], []
-        for r in range(G):
-            picked_plane = keep.tile([P, H], U8, align_bytes=64, name="w1_plane%d" % r)
-            nc.vector.tensor_copy(
-                out=picked_plane[:], in_=w1s_all[:].indirect(list1[:, r * LIST_COLS:(r + 1) * LIST_COLS])
-            )
-            w1_planes.append(picked_plane)
+        def pick(window, offsets, r, out):
+            nc.vector.tensor_copy(out=out, in_=window.indirect(offsets[:, r * LIST_COLS:(r + 1) * LIST_COLS]))
+
+        w1_plane = keep.tile([P, G * H], U8, align_bytes=64)
+        nc.vector.tensor_copy(out=w1_plane[:], in_=w1s_all[:].indirect(list1[:]))
+        w1_codes = []
         for r in range(G):
             picked = keep.tile([P, H], I32, align_bytes=64, name="w1_codes%d" % r)
-            nc.vector.tensor_copy(
-                out=picked[:].bitcast(U32),
-                in_=w1_all[:].bitcast(U32).indirect(list1[:, r * LIST_COLS:(r + 1) * LIST_COLS]),
-            )
+            pick(w1_all[:].bitcast(U32), list1, r, picked[:].bitcast(U32))
             w1_codes.append(picked)
-
-        w2s_picked = keep.tile([P, G * N], U8, align_bytes=64, tag="first_matrices")
-        nc.vector.tensor_copy(out=w2s_picked[:], in_=w2s_all[:].indirect(list2[:]))
-        w2_plane = keep.tile([P, G * N], U8, align_bytes=64)
-        nc.vector.tensor_copy(
-            out=w2_plane[:].rearrange("p (r j b i) -> p r b j i", r=G, j=PACK, i=16),
-            in_=w2s_picked[:].rearrange("p (r b i j) -> p r b j i", r=G, j=PACK, i=16),
-        )
 
         y_codes = keep.tile([P, T], I32, align_bytes=64)
         y_plane = keep.tile([P, T], U8, align_bytes=64)
@@ -121,13 +115,13 @@ def tile_moe_wsel_b_silu_p_kernel(
         for k, (half, r, cc) in enumerate(units):
             c = 2 * half + cc
             tokens = slice(c * P, (c + 1) * P)
-            pre = psum.tile([P, H], F32, tag="bank%d" % (k % 6))
+            pre = psum.tile([P, H], F32, tag="bank%d" % k)
             nc.tensor.matmul_mx(
                 out=pre[:],
                 lhsT=x_codes[:, tokens].bitcast(FP8X4),
                 lhsT_scale=x_plane[X_ROW:P, tokens],
                 rhs=w1_codes[r][:].bitcast(FP8X4),
-                rhs_scale=w1_planes[r][:],
+                rhs_scale=w1_plane[:, r * H:(r + 1) * H],
                 start=True,
                 stop=True,
             )
@@ -136,29 +130,36 @@ def tile_moe_wsel_b_silu_p_kernel(
                 out=act[:].rearrange("p (u m e) -> p u m e", u=2, e=2),
                 in_=pre[:].rearrange("p (m u e) -> p u m e", u=2, e=2),
                 func=SILU,
+                bias=no_bias[:] if k == 0 else 0.0,
             )
             acts[r, c] = act
+            if k == 0:
+                gate_cols = keep.tile([P, G * CHUNKS], F32, align_bytes=64, tag="gate_cols")
+                nc.scalar.copy(out=gate_cols[:], in_=gate_bank[:, 0:G * CHUNKS])
 
-        def apply_gate(half, r):
+        def apply_gate(half, r, rows):
             gated = []
             for cc in range(2):
                 c = 2 * half + cc
                 col = r * CHUNKS + c
-                tag = "first_matrices" if (r, c) == (0, 0) else "gated%d" % col
-                h_tok = keep.tile([P, H], BF16, align_bytes=64, tag=tag)
-                if half == 0:
+                h_tok = rows[:, cc * H:(cc + 1) * H]
+                if GATE_ENGINE[col] == "g":
+                    nc.gpsimd.tensor_scalar(
+                        out=h_tok, in0=acts[r, c][:], scalar1=gate_cols[:, col:col + 1], scalar2=0.0, op0=MULT, op1=ADD
+                    )
+                elif GATE_ENGINE[col] == "v":
                     nc.vector.tensor_scalar(
-                        out=h_tok[:], in0=acts[r, c][:], scalar1=gate_cols[:, col:col + 1], scalar2=None, op0=MULT
+                        out=h_tok, in0=acts[r, c][:], scalar1=gate_cols[:, col:col + 1], scalar2=None, op0=MULT
                     )
                 else:
-                    nc.scalar.activation(out=h_tok[:], in_=acts[r, c][:], func=COPY, scale=gate_cols[:, col:col + 1])
+                    nc.scalar.activation(out=h_tok, in_=acts[r, c][:], func=COPY, scale=gate_cols[:, col:col + 1])
                 gated.append(h_tok)
             return gated
 
-        def turn_and_quantize(r, gated):
-            turned = psum.tile([P, 2, 2, P], F32, tag="bank%d" % r)
+        def turn_and_quantize(bank, gated, codes):
+            turned = psum.tile([P, 2, 2, P], F32, tag="bank%d" % bank)
             for cc in range(2):
-                pairs = gated[cc][:].bitcast(F32)
+                pairs = gated[cc].bitcast(F32)
                 for u in range(2):
                     nc.tensor.transpose(turned[:, cc, u, :], pairs[:, u * P:(u + 1) * P], ident[:])
             h_grouped = ring.tile([P, 2 * P * PACK], BF16, align_bytes=64)
@@ -166,34 +167,38 @@ def tile_moe_wsel_b_silu_p_kernel(
                 out=h_grouped[:].bitcast(F32).rearrange("p (c t u) -> p c t u", c=2, u=2),
                 in_=turned[:].rearrange("p c u t -> p c t u"),
             )
-            codes = ring.tile([P, 2 * P], I32, align_bytes=64)
             plane = ring.tile([P, 2 * P], U8, align_bytes=64)
-            nc.vector.quantize_mx(out=codes[:].bitcast(FP8X4), scales=plane[:], in_=h_grouped[:])
+            nc.vector.quantize_mx(out=codes.bitcast(FP8X4), scales=plane[:], in_=h_grouped[:])
             return codes, plane
 
-        gated = {(0, r): apply_gate(0, r) for r in range(G)}
-        w2_picked = keep.tile([P, G * N], I32, align_bytes=64, tag="act3")
+        w2s_picked = keep.tile([P, G * N], U8, align_bytes=64, tag="first_matrices")
+        nc.vector.tensor_copy(out=w2s_picked[:], in_=w2s_all[:].indirect(list2[:]))
+        gated = {}
+        h_first = keep.tile([P, CHUNKS * H], BF16, align_bytes=64, tag="second_scales")
         for r in range(G):
-            nc.vector.tensor_copy(
-                out=w2_picked[:, r * N:(r + 1) * N].bitcast(U32),
-                in_=w2_all[:].bitcast(U32).indirect(list2[:, r * LIST_COLS:(r + 1) * LIST_COLS]),
-            )
+            gated[0, r] = apply_gate(0, r, h_first[:, 2 * r * H:2 * (r + 1) * H])
+        w2_plane = keep.tile([P, G * N], U8, align_bytes=64, tag="act2")
+        nc.vector.tensor_copy(
+            out=w2_plane[:].rearrange("p (r j b i) -> p r b j i", r=G, j=PACK, i=16),
+            in_=w2s_picked[:].rearrange("p (r b i j) -> p r b j i", r=G, j=PACK, i=16),
+        )
+        h_third = keep.tile([P, 2 * H], BF16, align_bytes=64, tag="first_matrices")
+        gated[1, 0] = apply_gate(1, 0, h_third[:])
+        h_last = keep.tile([P, 2 * H], BF16, align_bytes=64)
+        gated[1, 1] = apply_gate(1, 1, h_last[:])
+        w2_picked = keep.tile([P, G * N], I32, align_bytes=64, tag="act4")
+        nc.vector.tensor_copy(out=w2_picked[:].bitcast(U32), in_=w2_all[:].bitcast(U32).indirect(list2[:]))
+        w2_codes = keep.tile([P, G * N], I32, align_bytes=64)
+        nc.vector.tensor_copy(
+            out=w2_codes[:].rearrange("p (r j b i) -> p r b j i", r=G, j=PACK, i=4),
+            in_=w2_picked[:].rearrange("p (r b i j) -> p r b j i", r=G, j=PACK, i=4),
+        )
 
-        def deal(r, tag):
-            dealt = keep.tile([P, N], I32, align_bytes=64, tag=tag)
-            nc.vector.tensor_copy(
-                out=dealt[:].rearrange("p (j b i) -> p b j i", j=PACK, i=4),
-                in_=w2_picked[:, r * N:(r + 1) * N].rearrange("p (b i j) -> p b j i", j=PACK, i=4),
-            )
-            return dealt
-
-        w2_codes = [deal(0, "w2_codes0")]
-        gated[1, 0] = apply_gate(1, 0)
-        hq = {(0, r): turn_and_quantize(r, gated[0, r]) for r in range(G)}
-        gated[1, 1] = apply_gate(1, 1)
-        w2_codes.append(deal(1, "act7"))
-        for r in range(G):
-            hq[1, r] = turn_and_quantize(r, gated[1, r])
+        h_words = keep.tile([P, G * T], I32, align_bytes=64, tag="second_matrices")
+        hq = {}
+        for half in range(2):
+            for r in range(G):
+                hq[half, r] = turn_and_quantize(6 + r, gated[half, r], h_words[:, r * T + half * 2 * P:r * T + (half + 1) * 2 * P])
 
         for half in range(2):
             h_codes = [hq[half, r][0] for r in range(G)]
@@ -202,26 +207,31 @@ def tile_moe_wsel_b_silu_p_kernel(
                 c = 2 * half + cc
                 tokens = slice(c * P, (c + 1) * P)
                 local = slice(cc * P, (cc + 1) * P)
-                acc = psum.tile([P, PACK, P], F32, tag="bank%d" % (2 + c))
+                acc = psum.tile([P, PACK, P], F32, tag="bank%d" % (6, 1, 2, 3)[c])
                 for j in range(PACK):
                     for r in range(G):
                         nc.tensor.matmul_mx(
                             out=acc[:, j, :],
-                            lhsT=w2_codes[r][:, j * P:(j + 1) * P].bitcast(FP8X4),
+                            lhsT=w2_codes[:, r * N + j * P:r * N + (j + 1) * P].bitcast(FP8X4),
                             lhsT_scale=w2_plane[W2_ROW:P, r * N + j * P:r * N + (j + 1) * P],
                             rhs=h_codes[r][:, local].bitcast(FP8X4),
                             rhs_scale=h_planes[r][:, local],
                             start=(r == 0),
                             stop=(r == G - 1),
                         )
+                y_grouped = ring.tile([P, P * PACK], BF16, align_bytes=64)
+                if c == CHUNKS:
+                    nc.vector.tensor_copy(
+                        out=y_grouped[:].rearrange("p (t j) -> p t j", j=PACK), in_=acc[:].rearrange("p j t -> p t j")
+                    )
                 y = ring.tile([P, PACK * P], F32)
                 nc.scalar.copy(out=y[:], in_=acc[:].rearrange("p j t -> p (j t)"))
                 nc.sync.dma_start(out=out_rows[:, :, tokens], in_=y[:].rearrange("p (j t) -> p j t", j=PACK))
-                y_grouped = ring.tile([P, P * PACK], BF16, align_bytes=64)
-                nc.vector.tensor_copy(
-                    out=y_grouped[:].rearrange("p (b i j) -> p b j i", j=PACK, i=4),
-                    in_=y[:].rearrange("p (j b i) -> p b j i", j=PACK, i=4),
-                )
+                if c < CHUNKS:
+                    nc.vector.tensor_copy(
+                        out=y_grouped[:].rearrange("p (b i j) -> p b j i", j=PACK, i=4),
+                        in_=y[:].rearrange("p (j b i) -> p b j i", j=PACK, i=4),
+                    )
                 nc.vector.quantize_mx(
                     out=y_codes[:, tokens].bitcast(FP8X4), scales=y_plane[:, tokens], in_=y_grouped[:]
                 )
@@ -230,5 +240,5 @@ def tile_moe_wsel_b_silu_p_kernel(
         for q in range(4):
             queue = nc.scalar if q % 2 else nc.sync
             queue.dma_start(
-                out=out_2[0, 4 * q:4 * q + 4, :].bitcast(I32), in_=y_plane[32 * q:32 * q + 4, :].bitcast(I32)
+                out=out_2[0, q:16:4, :].bitcast(I32), in_=y_plane[q:P:32, :].bitcast(I32)
             )

@@ -22,6 +22,7 @@ PACK = 4
 CHUNKS = T // P
 LIST_COLS = H // 16
 X_ROW = 8
+HALF = T // 2
 EARLY = 1024
 GATE_ENGINE = "vvvvvvss"
 W2_ROW = 4
@@ -156,13 +157,13 @@ def tile_moe_wsel_b_silu_p_kernel(
                 gated.append(h_tok)
             return gated
 
-        def turn_and_quantize(bank, gated, codes):
+        def turn_and_quantize(bank, gated, codes, tag):
             turned = psum.tile([P, 2, 2, P], F32, tag="bank%d" % bank)
             for cc in range(2):
                 pairs = gated[cc].bitcast(F32)
                 for u in range(2):
                     nc.tensor.transpose(turned[:, cc, u, :], pairs[:, u * P:(u + 1) * P], ident[:])
-            h_grouped = ring.tile([P, 2 * P * PACK], BF16, align_bytes=64)
+            h_grouped = keep.tile([P, 2 * P * PACK], BF16, align_bytes=64, tag=tag)
             nc.scalar.copy(
                 out=h_grouped[:].bitcast(F32).rearrange("p (c t u) -> p c t u", c=2, u=2),
                 in_=turned[:].rearrange("p c u t -> p c t u"),
@@ -184,61 +185,77 @@ def tile_moe_wsel_b_silu_p_kernel(
         )
         h_third = keep.tile([P, 2 * H], BF16, align_bytes=64, tag="first_matrices")
         gated[1, 0] = apply_gate(1, 0, h_third[:])
-        h_last = keep.tile([P, 2 * H], BF16, align_bytes=64)
-        gated[1, 1] = apply_gate(1, 1, h_last[:])
-        w2_picked = keep.tile([P, G * N], I32, align_bytes=64, tag="act4")
-        nc.vector.tensor_copy(out=w2_picked[:].bitcast(U32), in_=w2_all[:].bitcast(U32).indirect(list2[:]))
-        w2_codes = keep.tile([P, G * N], I32, align_bytes=64)
-        nc.vector.tensor_copy(
-            out=w2_codes[:].rearrange("p (r j b i) -> p r b j i", r=G, j=PACK, i=4),
-            in_=w2_picked[:].rearrange("p (r b i j) -> p r b j i", r=G, j=PACK, i=4),
-        )
 
-        h_words = keep.tile([P, G * T], I32, align_bytes=64, tag="second_matrices")
+        def pick_dealt(r, tag):
+            dealt = keep.tile([P, N], I32, align_bytes=64, tag=tag)
+            pick(w2_all[:].bitcast(U32), list2, r, dealt[:].bitcast(U32).rearrange("p (j m) -> p m j", j=PACK))
+            return dealt
+
         hq = {}
-        for half in range(2):
-            for r in range(G):
-                hq[half, r] = turn_and_quantize(6 + r, gated[half, r], h_words[:, r * T + half * 2 * P:r * T + (half + 1) * 2 * P])
+        w2_codes = [pick_dealt(0, "act4")]
+        h_first_words = keep.tile([P, HALF], I32, align_bytes=64)
+        hq[0, 0] = turn_and_quantize(0, gated[0, 0], h_first_words[:], "grouped0")
+        w2_codes.append(pick_dealt(1, "grouped0"))
+        h_words = keep.tile([P, 3 * HALF], I32, align_bytes=64, tag="second_matrices")
+        hq[0, 1] = turn_and_quantize(5, gated[0, 1], h_words[:, 0:HALF], "grouped1")
+        h_last = keep.tile([P, 2 * H], BF16, align_bytes=64, tag="second_scales")
+        gated[1, 1] = apply_gate(1, 1, h_last[:])
+        for r in range(G):
+            hq[1, r] = turn_and_quantize(
+                6 + r, gated[1, r], h_words[:, (1 + r) * HALF:(2 + r) * HALF], "grouped%d" % (2 + r)
+            )
 
-        for half in range(2):
-            h_codes = [hq[half, r][0] for r in range(G)]
-            h_planes = [hq[half, r][1] for r in range(G)]
-            for cc in range(2):
-                c = 2 * half + cc
-                tokens = slice(c * P, (c + 1) * P)
-                local = slice(cc * P, (cc + 1) * P)
-                acc = psum.tile([P, PACK, P], F32, tag="bank%d" % (6, 1, 2, 3)[c])
-                for j in range(PACK):
-                    for r in range(G):
-                        nc.tensor.matmul_mx(
-                            out=acc[:, j, :],
-                            lhsT=w2_codes[:, r * N + j * P:r * N + (j + 1) * P].bitcast(FP8X4),
-                            lhsT_scale=w2_plane[W2_ROW:P, r * N + j * P:r * N + (j + 1) * P],
-                            rhs=h_codes[r][:, local].bitcast(FP8X4),
-                            rhs_scale=h_planes[r][:, local],
-                            start=(r == 0),
-                            stop=(r == G - 1),
-                        )
-                y_grouped = ring.tile([P, P * PACK], BF16, align_bytes=64)
-                if c == CHUNKS:
-                    nc.vector.tensor_copy(
-                        out=y_grouped[:].rearrange("p (t j) -> p t j", j=PACK), in_=acc[:].rearrange("p j t -> p t j")
-                    )
-                y = ring.tile([P, PACK * P], F32)
-                nc.scalar.copy(out=y[:], in_=acc[:].rearrange("p j t -> p (j t)"))
-                nc.sync.dma_start(out=out_rows[:, :, tokens], in_=y[:].rearrange("p (j t) -> p j t", j=PACK))
-                if c < CHUNKS:
-                    nc.vector.tensor_copy(
-                        out=y_grouped[:].rearrange("p (b i j) -> p b j i", j=PACK, i=4),
-                        in_=y[:].rearrange("p (j b i) -> p b j i", j=PACK, i=4),
-                    )
-                nc.vector.quantize_mx(
-                    out=y_codes[:, tokens].bitcast(FP8X4), scales=y_plane[:, tokens], in_=y_grouped[:]
-                )
-                nc.sync.dma_start(out=out_words[:, tokens], in_=y_codes[:, tokens])
+        def second_layer_pass(out, half, r, j):
+            nc.tensor.matmul_mx(
+                out=out,
+                lhsT=w2_codes[r][:, j * P:(j + 1) * P].bitcast(FP8X4),
+                lhsT_scale=w2_plane[W2_ROW:P, r * N + j * P:r * N + (j + 1) * P],
+                rhs=hq[half, r][0].bitcast(FP8X4),
+                rhs_scale=hq[half, r][1][:],
+                start=(r == 0),
+                stop=(r == G - 1),
+            )
+
+        def round_and_group(engine, y_rows, name):
+            grouped = keep.tile([P, PACK * y_rows.shape[2]], BF16, align_bytes=64, name=name)
+            engine(
+                out=grouped[:].rearrange("p (b i j) -> p b j i", j=PACK, i=4),
+                in_=y_rows.rearrange("p j (b i) -> p b j i", i=4),
+            )
+            return grouped
+
+        def quantize_and_store(grouped, tokens):
+            nc.vector.quantize_mx(out=y_codes[:, tokens].bitcast(FP8X4), scales=y_plane[:, tokens], in_=grouped[:])
+
+        sums = [psum.tile([P, HALF], F32, tag="bank%d" % (6, 1, 2, 3)[j], name="sums%d" % j) for j in range(PACK)]
+        for r in range(G):
+            for j in range(PACK):
+                second_layer_pass(sums[j][:], 0, r, j)
+        y_first = keep.tile([P, PACK, HALF], F32, align_bytes=64)
+        for j in range(PACK):
+            engine = nc.scalar.copy if j < 2 else nc.vector.tensor_copy
+            engine(out=y_first[:, j, :], in_=sums[j][:])
+            if j % 2:
+                nc.sync.dma_start(out=out_rows[:, j - 1:j + 1, 0:HALF], in_=y_first[:, j - 1:j + 1, :])
+
+        y_second = keep.tile([P, PACK, HALF], F32, align_bytes=64)
+        for pair in range(2):
+            both = psum.tile([P, 2, HALF], F32, tag="bank%d" % (5 * pair))
+            for jj in range(2):
+                for r in range(G):
+                    second_layer_pass(both[:, jj, :], 1, r, 2 * pair + jj)
+            nc.scalar.copy(out=y_second[:, 2 * pair:2 * pair + 2, :], in_=both[:])
+            nc.sync.dma_start(out=out_rows[:, 2 * pair:2 * pair + 2, HALF:T], in_=y_second[:, 2 * pair:2 * pair + 2, :])
+
+        grouped = round_and_group(nc.vector.tensor_copy, y_first[:], "grouped_first")
+        quantize_and_store(grouped, slice(0, HALF))
+        nc.sync.dma_start(out=out_words[:, 0:HALF], in_=y_codes[:, 0:HALF])
+        grouped2 = round_and_group(nc.vector.tensor_copy, y_second[:, :, 0:P], "grouped_third")
+        grouped3 = round_and_group(nc.scalar.copy, y_second[:, :, P:HALF], "grouped_last")
+        quantize_and_store(grouped2, slice(HALF, HALF + P))
+        quantize_and_store(grouped3, slice(HALF + P, T))
+        nc.sync.dma_start(out=out_words[:, HALF:T], in_=y_codes[:, HALF:T])
 
         for q in range(4):
             queue = nc.scalar if q % 2 else nc.sync
-            queue.dma_start(
-                out=out_2[0, q:16:4, :].bitcast(I32), in_=y_plane[q:P:32, :].bitcast(I32)
-            )
+            queue.dma_start(out=out_2[0, q:16:4, :].bitcast(I32), in_=y_plane[q:P:32, :].bitcast(I32))

@@ -25,7 +25,6 @@ X_ROW = 8
 HALF = T // 2
 EARLY = 1024
 GATE_ENGINE = "vvvvvvss"
-W2_ROW = 4
 
 
 def load_scale_rows(queues, plane, scales, first_row):
@@ -46,6 +45,7 @@ def tile_moe_wsel_b_silu_p_kernel(
     with ExitStack() as ctx:
         keep = ctx.enter_context(tc.tile_pool(name="keep", bufs=1))
         ring = ctx.enter_context(tc.tile_pool(name="ring", bufs=8))
+        placed = ctx.enter_context(tc.tile_pool(name="placed", bufs=1))
         psum = ctx.enter_context(tc.psum_pool(name="psum", bufs=1))
 
         list1 = keep.tile([P, G * LIST_COLS], U16)
@@ -54,15 +54,16 @@ def tile_moe_wsel_b_silu_p_kernel(
         w2s_all = keep.tile([P, E * N], U8, align_bytes=64, tag="second_scales")
         x_plane = keep.tile([P, T], U8, align_bytes=64)
         w1_all = keep.tile([P, E * H], I32, align_bytes=64, tag="first_matrices")
-        zeros2 = keep.tile([P, P], F32, align_bytes=64, tag="tokens")
-        gate_rows = keep.tile([P, P], F32, align_bytes=64, tag="second_matrices")
+        zeros2 = placed.tile([P, P], F32, align_bytes=64, offset=2048 - 256)
+        gate_rows = keep.tile([P, P], F32, align_bytes=64)
         ident = keep.tile([P, P], F32)
 
         nc.gpsimd.memset(w1s_all[:, 0:E * H // 2].bitcast(I32), 0)
         nc.gpsimd.memset(w1_all[:, EARLY:EARLY + P], 0)
-        nc.gpsimd.memset(zeros2[:], 0.0)
         nc.gpsimd.memset(gate_rows[:], 0.0)
         gate_runs = gate.rearrange("r q (c p) -> (r q c) p", p=P)
+        nc.gpsimd.dma_start(out=gate_rows[0:G * CHUNKS, :], in_=gate_runs[0:G * P * CHUNKS:P + 1, :])
+        nc.gpsimd.memset(zeros2[:], 0.0)
         nc.gpsimd.affine_select(
             out=ident[:],
             in_=zeros2[:],
@@ -85,14 +86,13 @@ def tile_moe_wsel_b_silu_p_kernel(
         nc.sync.dma_start(out=w1_all[:, 0:EARLY], in_=words_of(w1_words)[:, 0:EARLY])
         load_scale_rows([nc.sync], w1s_all, w1_scales, 0)
         nc.sync.dma_start(out=w1_all[:, EARLY:E * H], in_=words_of(w1_words)[:, EARLY:E * H])
-        nc.sync.dma_start(out=gate_rows[0:G * CHUNKS, :], in_=gate_runs[0:G * P * CHUNKS:P + 1, :])
-        x_codes = keep.tile([P, T], I32, align_bytes=64, tag="tokens")
+        x_codes = placed.tile([P, T], I32, align_bytes=64, offset=0)
         nc.sync.dma_start(out=x_codes[:], in_=words_of(x_words))
         load_scale_rows([nc.sync], x_plane, x_scales, X_ROW)
-        load_scale_rows([nc.sync], w2s_all, w2_scales, W2_ROW)
+        nc.sync.dma_start(out=w2s_all[0:P:8, :].bitcast(I32), in_=w2_scales[0].bitcast(I32))
         gate_bank = psum.tile([P, P], F32, tag="bank7")
         nc.tensor.transpose(gate_bank[:], gate_rows[:], ident[:])
-        w2_all = keep.tile([P, E * N], I32, align_bytes=64, tag="second_matrices")
+        w2_all = placed.tile([P, E * N], I32, align_bytes=64, offset=2048)
         nc.sync.dma_start(out=w2_all[:], in_=words_of(w2_words))
 
         def pick(window, offsets, r, out):
@@ -183,6 +183,8 @@ def tile_moe_wsel_b_silu_p_kernel(
             out=w2_plane[:].rearrange("p (r j b i) -> p r b j i", r=G, j=PACK, i=16),
             in_=w2s_picked[:].rearrange("p (r b i j) -> p r b j i", r=G, j=PACK, i=16),
         )
+        for q in range(1, 4):
+            nc.sync.dma_start(out=w2_plane[q:P:32, :].bitcast(I32), in_=w2_plane[8 * q:P:32, :].bitcast(I32))
         h_third = keep.tile([P, 2 * H], BF16, align_bytes=64, tag="first_matrices")
         gated[1, 0] = apply_gate(1, 0, h_third[:])
 
@@ -196,7 +198,7 @@ def tile_moe_wsel_b_silu_p_kernel(
         h_first_words = keep.tile([P, HALF], I32, align_bytes=64)
         hq[0, 0] = turn_and_quantize(0, gated[0, 0], h_first_words[:], "grouped0")
         w2_codes.append(pick_dealt(1, "grouped0"))
-        h_words = keep.tile([P, 3 * HALF], I32, align_bytes=64, tag="second_matrices")
+        h_words = placed.tile([P, 3 * HALF], I32, align_bytes=64, offset=2048)
         hq[0, 1] = turn_and_quantize(5, gated[0, 1], h_words[:, 0:HALF], "grouped1")
         h_last = keep.tile([P, 2 * H], BF16, align_bytes=64, tag="second_scales")
         gated[1, 1] = apply_gate(1, 1, h_last[:])
@@ -209,7 +211,7 @@ def tile_moe_wsel_b_silu_p_kernel(
             nc.tensor.matmul_mx(
                 out=out,
                 lhsT=w2_codes[r][:, j * P:(j + 1) * P].bitcast(FP8X4),
-                lhsT_scale=w2_plane[W2_ROW:P, r * N + j * P:r * N + (j + 1) * P],
+                lhsT_scale=w2_plane[:, r * N + j * P:r * N + (j + 1) * P],
                 rhs=hq[half, r][0].bitcast(FP8X4),
                 rhs_scale=hq[half, r][1][:],
                 start=(r == 0),

@@ -15,7 +15,6 @@ FP8X4 = mybir.dt.float8_e4m3fn_x4
 SILU = mybir.ActivationFunctionType.Silu
 COPY = mybir.ActivationFunctionType.Copy
 MULT = mybir.AluOpType.mult
-ADD = mybir.AluOpType.add
 
 P = 128
 PACK = 4
@@ -23,8 +22,8 @@ CHUNKS = T // P
 LIST_COLS = H // 16
 X_ROW = 8
 HALF = T // 2
-EARLY = 1024
-GATE_ENGINE = "vvvvvvss"
+KB = 1024
+EARLY = 768
 
 
 def load_scale_rows(queues, plane, scales, first_row):
@@ -44,55 +43,68 @@ def tile_moe_wsel_b_silu_p_kernel(
     nc = tc.nc
     with ExitStack() as ctx:
         keep = ctx.enter_context(tc.tile_pool(name="keep", bufs=1))
-        ring = ctx.enter_context(tc.tile_pool(name="ring", bufs=8))
         placed = ctx.enter_context(tc.tile_pool(name="placed", bufs=1))
         psum = ctx.enter_context(tc.psum_pool(name="psum", bufs=1))
 
+        def at(offset, shape, dtype, name):
+            return placed.tile(shape, dtype, align_bytes=64, offset=offset, name=name)
+
+        X_AT = 0
+        GATE_AT = 2 * KB
+        W2_AT = 2 * KB + 512
+        DEALT_AT = (16 * KB, 18 * KB)
+        LAST_AT = 20 * KB
+        ROUND_AT = 22 * KB
+
         list1 = keep.tile([P, G * LIST_COLS], U16)
         list2 = keep.tile([P, G * LIST_COLS], U16)
-        w1s_all = keep.tile([P, E * H], U8, align_bytes=64, tag="first_scales")
-        w2s_all = keep.tile([P, E * N], U8, align_bytes=64, tag="second_scales")
+        w1s_all = keep.tile([P, E * H], U8, align_bytes=64)
+        w2s_all = keep.tile([P, E * N], U8, align_bytes=64)
         x_plane = keep.tile([P, T], U8, align_bytes=64)
-        w1_all = keep.tile([P, E * H], I32, align_bytes=64, tag="first_matrices")
-        zeros2 = placed.tile([P, P], F32, align_bytes=64, offset=2048 - 256)
-        gate_rows = keep.tile([P, P], F32, align_bytes=64)
+        w1_all = keep.tile([P, E * H], I32, align_bytes=64)
+        zeros = at(GATE_AT - 64, [P, P + 32], F32, "zeros")
         ident = keep.tile([P, P], F32)
+        zero_col = keep.tile([P, 1], F32, align_bytes=64)
+        biases = {
+            0: keep.tile([P, 1], F32, align_bytes=64, name="bias0"),
+            3: at(DEALT_AT[0], [P, 1], F32, "bias3"),
+            6: at(DEALT_AT[1], [P, 1], F32, "bias6"),
+        }
 
         nc.gpsimd.memset(w1s_all[:, 0:E * H // 2].bitcast(I32), 0)
         nc.gpsimd.memset(w1_all[:, EARLY:EARLY + P], 0)
-        nc.gpsimd.memset(gate_rows[:], 0.0)
-        gate_runs = gate.rearrange("r q (c p) -> (r q c) p", p=P)
-        nc.gpsimd.dma_start(out=gate_rows[0:G * CHUNKS, :], in_=gate_runs[0:G * P * CHUNKS:P + 1, :])
-        nc.gpsimd.memset(zeros2[:], 0.0)
+        nc.gpsimd.memset(zero_col[:], 0.0)
+        nc.gpsimd.memset(w2s_all[:].bitcast(I32), 0)
+        nc.gpsimd.memset(biases[3][:], 0.0)
+        nc.gpsimd.memset(biases[6][:], 0.0)
+        nc.scalar.activation(out=biases[0][:, 0:1], in_=zero_col[:], func=SILU)
+        nc.vector.memset(w1s_all[:, E * H // 2:E * H].bitcast(I32), 0)
+        nc.vector.tensor_copy(out=x_plane[:].bitcast(I32), in_=w1_all[:, EARLY:EARLY + P])
+        nc.vector.memset(zeros[:, 0:P], 0.0)
         nc.gpsimd.affine_select(
             out=ident[:],
-            in_=zeros2[:],
+            in_=zeros[:, 0:P],
             compare_op=mybir.AluOpType.not_equal,
             fill=1.0,
             base=0,
             pattern=[[-1, P]],
             channel_multiplier=1,
         )
-        no_bias = keep.tile([P, 1], F32, align_bytes=64, tag="gate_cols")
-        zero_col = keep.tile([P, 1], F32, align_bytes=64)
-        nc.gpsimd.memset(zero_col[:], 0.0)
-        nc.scalar.activation(out=no_bias[:], in_=zero_col[:], func=SILU)
-        nc.vector.memset(w1s_all[:, E * H // 2:E * H].bitcast(I32), 0)
-        nc.vector.tensor_copy(out=x_plane[:].bitcast(I32), in_=w1_all[:, EARLY:EARLY + P])
-        nc.vector.memset(w2s_all[:].bitcast(I32), 0)
+        gate_rows = at(GATE_AT, [P, P], F32, "gate_rows")
+        nc.gpsimd.memset(gate_rows[:], 0.0)
+        gate_runs = gate.rearrange("r q (c p) -> (r q c) p", p=P)
+        nc.gpsimd.dma_start(out=gate_rows[0:G * CHUNKS, :], in_=gate_runs[0:G * P * CHUNKS:P + 1, :])
 
         nc.sync.dma_start(list1[:], offs)
         nc.sync.dma_start(list2[:], offs2)
         nc.sync.dma_start(out=w1_all[:, 0:EARLY], in_=words_of(w1_words)[:, 0:EARLY])
         load_scale_rows([nc.sync], w1s_all, w1_scales, 0)
         nc.sync.dma_start(out=w1_all[:, EARLY:E * H], in_=words_of(w1_words)[:, EARLY:E * H])
-        x_codes = placed.tile([P, T], I32, align_bytes=64, offset=0)
-        nc.sync.dma_start(out=x_codes[:], in_=words_of(x_words))
         load_scale_rows([nc.sync], x_plane, x_scales, X_ROW)
+        x_codes = at(X_AT, [P, T], I32, "x_codes")
+        nc.sync.dma_start(out=x_codes[:], in_=words_of(x_words))
         nc.sync.dma_start(out=w2s_all[0:P:8, :].bitcast(I32), in_=w2_scales[0].bitcast(I32))
-        gate_bank = psum.tile([P, P], F32, tag="bank7")
-        nc.tensor.transpose(gate_bank[:], gate_rows[:], ident[:])
-        w2_all = placed.tile([P, E * N], I32, align_bytes=64, offset=2048)
+        w2_all = at(W2_AT, [P, E * N], I32, "w2_all")
         nc.sync.dma_start(out=w2_all[:], in_=words_of(w2_words))
 
         def pick(window, offsets, r, out):
@@ -113,9 +125,10 @@ def tile_moe_wsel_b_silu_p_kernel(
 
         units = [(half, r, cc) for half in range(2) for r in range(G) for cc in range(2)]
         acts = {}
-        for k, (half, r, cc) in enumerate(units):
-            c = 2 * half + cc
-            tokens = slice(c * P, (c + 1) * P)
+
+        def first_layer(k):
+            half, r, cc = units[k]
+            tokens = slice((2 * half + cc) * P, (2 * half + cc + 1) * P)
             pre = psum.tile([P, H], F32, tag="bank%d" % k)
             nc.tensor.matmul_mx(
                 out=pre[:],
@@ -126,137 +139,145 @@ def tile_moe_wsel_b_silu_p_kernel(
                 start=True,
                 stop=True,
             )
-            act = keep.tile([P, H], F32, align_bytes=64, tag="act%d" % k)
+            act = keep.tile([P, H], F32, align_bytes=64, name="act%d" % k)
             nc.scalar.activation(
                 out=act[:].rearrange("p (u m e) -> p u m e", u=2, e=2),
                 in_=pre[:].rearrange("p (m u e) -> p u m e", u=2, e=2),
                 func=SILU,
-                bias=no_bias[:] if k == 0 else 0.0,
+                bias=biases[k][:, 0:1] if k in biases else 0.0,
             )
-            acts[r, c] = act
-            if k == 0:
-                gate_cols = keep.tile([P, G * CHUNKS], F32, align_bytes=64, tag="gate_cols")
-                nc.scalar.copy(out=gate_cols[:], in_=gate_bank[:, 0:G * CHUNKS])
+            acts[k] = act
 
-        def apply_gate(half, r, rows):
-            gated = []
-            for cc in range(2):
-                c = 2 * half + cc
-                col = r * CHUNKS + c
-                h_tok = rows[:, cc * H:(cc + 1) * H]
-                if GATE_ENGINE[col] == "g":
-                    nc.gpsimd.tensor_scalar(
-                        out=h_tok, in0=acts[r, c][:], scalar1=gate_cols[:, col:col + 1], scalar2=0.0, op0=MULT, op1=ADD
-                    )
-                elif GATE_ENGINE[col] == "v":
-                    nc.vector.tensor_scalar(
-                        out=h_tok, in0=acts[r, c][:], scalar1=gate_cols[:, col:col + 1], scalar2=None, op0=MULT
-                    )
-                else:
-                    nc.scalar.activation(out=h_tok, in_=acts[r, c][:], func=COPY, scale=gate_cols[:, col:col + 1])
-                gated.append(h_tok)
-            return gated
+        gated = [keep.tile([P, 2 * H], BF16, align_bytes=64, name="gated%d" % i) for i in range(3)]
 
-        def turn_and_quantize(bank, gated, codes, tag):
-            turned = psum.tile([P, 2, 2, P], F32, tag="bank%d" % bank)
+        def apply_gate(k, on_scalar):
+            half, r, cc = units[k]
+            col = r * CHUNKS + 2 * half + cc
+            h_tok = gated[k // 2][:, cc * H:(cc + 1) * H]
+            if on_scalar:
+                nc.scalar.activation(out=h_tok, in_=acts[k][:], func=COPY, scale=gate_cols[:, col:col + 1])
+            else:
+                nc.vector.tensor_scalar(
+                    out=h_tok, in0=acts[k][:], scalar1=gate_cols[:, col:col + 1], scalar2=None, op0=MULT
+                )
+
+        def turn(i):
+            turned = psum.tile([P, 2, 2, P], F32, tag="bank%d" % i)
+            pairs = gated[i][:].bitcast(F32)
             for cc in range(2):
-                pairs = gated[cc].bitcast(F32)
                 for u in range(2):
-                    nc.tensor.transpose(turned[:, cc, u, :], pairs[:, u * P:(u + 1) * P], ident[:])
-            h_grouped = keep.tile([P, 2 * P * PACK], BF16, align_bytes=64, tag=tag)
+                    nc.tensor.transpose(turned[:, cc, u, :], pairs[:, (2 * cc + u) * P:(2 * cc + u + 1) * P], ident[:])
+            grouped = keep.tile([P, 2 * P * PACK], BF16, align_bytes=64, name="h_grouped%d" % i)
             nc.scalar.copy(
-                out=h_grouped[:].bitcast(F32).rearrange("p (c t u) -> p c t u", c=2, u=2),
+                out=grouped[:].bitcast(F32).rearrange("p (c t u) -> p c t u", c=2, u=2),
                 in_=turned[:].rearrange("p c u t -> p c t u"),
             )
-            plane = ring.tile([P, 2 * P], U8, align_bytes=64)
-            nc.vector.quantize_mx(out=codes.bitcast(FP8X4), scales=plane[:], in_=h_grouped[:])
+            return grouped
+
+        def quantize_hidden(i, grouped, codes):
+            plane = keep.tile([P, HALF], U8, align_bytes=64, name="h_plane%d" % i)
+            nc.vector.quantize_mx(out=codes[:].bitcast(FP8X4), scales=plane[:], in_=grouped[:])
             return codes, plane
 
-        w2s_picked = keep.tile([P, G * N], U8, align_bytes=64, tag="first_matrices")
+        def pick_dealt(r):
+            dealt = at(DEALT_AT[r], [P, N], I32, "w2_codes%d" % r)
+            pick(w2_all[:].bitcast(U32), list2, r, dealt[:].bitcast(U32).rearrange("p (j m) -> p m j", j=PACK))
+            return dealt
+
+        first_layer(0)
+        first_layer(1)
+        gate_bank = psum.tile([P, P], F32, tag="bank0")
+        nc.tensor.transpose(gate_bank[:], gate_rows[:], ident[:])
+        gate_cols = keep.tile([P, G * CHUNKS], F32, align_bytes=64)
+        nc.scalar.copy(out=gate_cols[:], in_=gate_bank[:, 0:G * CHUNKS])
+        for k in range(2, 6):
+            first_layer(k)
+
+        w2s_picked = keep.tile([P, G * N], U8, align_bytes=64)
         nc.vector.tensor_copy(out=w2s_picked[:], in_=w2s_all[:].indirect(list2[:]))
-        gated = {}
-        h_first = keep.tile([P, CHUNKS * H], BF16, align_bytes=64, tag="second_scales")
-        for r in range(G):
-            gated[0, r] = apply_gate(0, r, h_first[:, 2 * r * H:2 * (r + 1) * H])
-        w2_plane = keep.tile([P, G * N], U8, align_bytes=64, tag="act2")
+        apply_gate(0, False)
+        w2_plane = keep.tile([P, G * N], U8, align_bytes=64)
         nc.vector.tensor_copy(
             out=w2_plane[:].rearrange("p (r j b i) -> p r b j i", r=G, j=PACK, i=16),
             in_=w2s_picked[:].rearrange("p (r b i j) -> p r b j i", r=G, j=PACK, i=16),
         )
         for q in range(1, 4):
             nc.sync.dma_start(out=w2_plane[q:P:32, :].bitcast(I32), in_=w2_plane[8 * q:P:32, :].bitcast(I32))
-        h_third = keep.tile([P, 2 * H], BF16, align_bytes=64, tag="first_matrices")
-        gated[1, 0] = apply_gate(1, 0, h_third[:])
+        for k in range(1, 4):
+            apply_gate(k, False)
+        w2_codes = [pick_dealt(0)]
+        for k in range(4, 6):
+            apply_gate(k, False)
 
-        def pick_dealt(r, tag):
-            dealt = keep.tile([P, N], I32, align_bytes=64, tag=tag)
-            pick(w2_all[:].bitcast(U32), list2, r, dealt[:].bitcast(U32).rearrange("p (j m) -> p m j", j=PACK))
-            return dealt
+        grouped = [turn(0)]
+        for k in range(6, 8):
+            first_layer(k)
+        grouped.append(turn(1))
+        h_codes = [keep.tile([P, HALF], I32, align_bytes=64, name="h_codes%d" % i) for i in range(2)]
+        hq = [quantize_hidden(0, grouped[0], h_codes[0])]
+        gated.append(at(LAST_AT, [P, 2 * H], BF16, "gated3"))
+        apply_gate(6, False)
+        w2_codes.append(pick_dealt(1))
+        apply_gate(7, True)
+        grouped.append(turn(2))
+        grouped.append(turn(3))
+        hq.append(quantize_hidden(1, grouped[1], at(LAST_AT, [P, HALF], I32, "h_codes_held")))
+        hq.append(quantize_hidden(2, grouped[2], h_codes[1]))
+        hq.append(quantize_hidden(3, grouped[3], at(ROUND_AT, [P, HALF], I32, "h_codes_last")))
 
-        hq = {}
-        w2_codes = [pick_dealt(0, "act4")]
-        h_first_words = keep.tile([P, HALF], I32, align_bytes=64)
-        hq[0, 0] = turn_and_quantize(0, gated[0, 0], h_first_words[:], "grouped0")
-        w2_codes.append(pick_dealt(1, "grouped0"))
-        h_words = placed.tile([P, 3 * HALF], I32, align_bytes=64, offset=2048)
-        hq[0, 1] = turn_and_quantize(5, gated[0, 1], h_words[:, 0:HALF], "grouped1")
-        h_last = keep.tile([P, 2 * H], BF16, align_bytes=64, tag="second_scales")
-        gated[1, 1] = apply_gate(1, 1, h_last[:])
-        for r in range(G):
-            hq[1, r] = turn_and_quantize(
-                6 + r, gated[1, r], h_words[:, (1 + r) * HALF:(2 + r) * HALF], "grouped%d" % (2 + r)
-            )
+        def second_layer(half, first_bank):
+            sums = [
+                psum.tile([P, HALF], F32, tag="bank%d" % (first_bank + j), name="sums%d%d" % (half, j))
+                for j in range(PACK)
+            ]
+            for r in range(G):
+                codes, plane = hq[G * half + r]
+                for j in range(PACK):
+                    nc.tensor.matmul_mx(
+                        out=sums[j][:],
+                        lhsT=w2_codes[r][:, j * P:(j + 1) * P].bitcast(FP8X4),
+                        lhsT_scale=w2_plane[:, r * N + j * P:r * N + (j + 1) * P],
+                        rhs=codes[:].bitcast(FP8X4),
+                        rhs_scale=plane[:],
+                        start=(r == 0),
+                        stop=(r == G - 1),
+                    )
+            return sums
 
-        def second_layer_pass(out, half, r, j):
-            nc.tensor.matmul_mx(
-                out=out,
-                lhsT=w2_codes[r][:, j * P:(j + 1) * P].bitcast(FP8X4),
-                lhsT_scale=w2_plane[:, r * N + j * P:r * N + (j + 1) * P],
-                rhs=hq[half, r][0].bitcast(FP8X4),
-                rhs_scale=hq[half, r][1][:],
-                start=(r == 0),
-                stop=(r == G - 1),
-            )
+        def copy_out(half, sums, rows, j):
+            engine = nc.scalar.copy if j < 2 + half else nc.vector.tensor_copy
+            engine(out=rows[:, j, :], in_=sums[j][:])
+            if j % 2:
+                nc.sync.dma_start(
+                    out=out_rows[:, j - 1:j + 1, half * HALF:(half + 1) * HALF], in_=rows[:, j - 1:j + 1, :]
+                )
 
-        def round_and_group(engine, y_rows, name):
-            grouped = keep.tile([P, PACK * y_rows.shape[2]], BF16, align_bytes=64, name=name)
+        def round_and_group(engine, y_rows, out):
             engine(
-                out=grouped[:].rearrange("p (b i j) -> p b j i", j=PACK, i=4),
+                out=out.rearrange("p (b i j) -> p b j i", j=PACK, i=4),
                 in_=y_rows.rearrange("p j (b i) -> p b j i", i=4),
             )
-            return grouped
 
-        def quantize_and_store(grouped, tokens):
-            nc.vector.quantize_mx(out=y_codes[:, tokens].bitcast(FP8X4), scales=y_plane[:, tokens], in_=grouped[:])
+        def quantize_result(half, rounded):
+            tokens = slice(half * HALF, (half + 1) * HALF)
+            nc.vector.quantize_mx(out=y_codes[:, tokens].bitcast(FP8X4), scales=y_plane[:, tokens], in_=rounded[:])
+            nc.sync.dma_start(out=out_words[:, tokens], in_=y_codes[:, tokens])
 
-        sums = [psum.tile([P, HALF], F32, tag="bank%d" % (6, 1, 2, 3)[j], name="sums%d" % j) for j in range(PACK)]
-        for r in range(G):
-            for j in range(PACK):
-                second_layer_pass(sums[j][:], 0, r, j)
-        y_first = keep.tile([P, PACK, HALF], F32, align_bytes=64)
+        sums = [second_layer(0, 4), second_layer(1, 0)]
+        y = [keep.tile([P, PACK, HALF], F32, align_bytes=64, name="y%d" % half) for half in range(2)]
+        rounded = [
+            at(ROUND_AT, [P, PACK * HALF], BF16, "rounded0"),
+            keep.tile([P, PACK * HALF], BF16, align_bytes=64, name="rounded1"),
+        ]
         for j in range(PACK):
-            engine = nc.scalar.copy if j < 2 else nc.vector.tensor_copy
-            engine(out=y_first[:, j, :], in_=sums[j][:])
-            if j % 2:
-                nc.sync.dma_start(out=out_rows[:, j - 1:j + 1, 0:HALF], in_=y_first[:, j - 1:j + 1, :])
-
-        y_second = keep.tile([P, PACK, HALF], F32, align_bytes=64)
-        for pair in range(2):
-            both = psum.tile([P, 2, HALF], F32, tag="bank%d" % (5 * pair))
-            for jj in range(2):
-                for r in range(G):
-                    second_layer_pass(both[:, jj, :], 1, r, 2 * pair + jj)
-            nc.scalar.copy(out=y_second[:, 2 * pair:2 * pair + 2, :], in_=both[:])
-            nc.sync.dma_start(out=out_rows[:, 2 * pair:2 * pair + 2, HALF:T], in_=y_second[:, 2 * pair:2 * pair + 2, :])
-
-        grouped = round_and_group(nc.vector.tensor_copy, y_first[:], "grouped_first")
-        quantize_and_store(grouped, slice(0, HALF))
-        nc.sync.dma_start(out=out_words[:, 0:HALF], in_=y_codes[:, 0:HALF])
-        grouped2 = round_and_group(nc.vector.tensor_copy, y_second[:, :, 0:P], "grouped_third")
-        grouped3 = round_and_group(nc.scalar.copy, y_second[:, :, P:HALF], "grouped_last")
-        quantize_and_store(grouped2, slice(HALF, HALF + P))
-        quantize_and_store(grouped3, slice(HALF + P, T))
-        nc.sync.dma_start(out=out_words[:, HALF:T], in_=y_codes[:, HALF:T])
+            copy_out(0, sums[0], y[0], j)
+        for j in range(PACK):
+            copy_out(1, sums[1], y[1], j)
+        round_and_group(nc.vector.tensor_copy, y[0][:], rounded[0][:])
+        round_and_group(nc.vector.tensor_copy, y[1][:, :, 0:P], rounded[1][:, 0:PACK * P])
+        round_and_group(nc.scalar.copy, y[1][:, :, P:HALF], rounded[1][:, PACK * P:PACK * HALF])
+        quantize_result(0, rounded[0])
+        quantize_result(1, rounded[1])
 
         for q in range(4):
             queue = nc.scalar if q % 2 else nc.sync

@@ -50,8 +50,7 @@ def tile_moe_wsel_b_silu_p_kernel(
             return placed.tile(shape, dtype, align_bytes=64, offset=offset, name=name)
 
         X_AT = 0
-        GATE_AT = 2 * KB
-        W2_AT = 2 * KB + 512
+        W2_AT = 2 * KB
         DEALT_AT = (16 * KB, 18 * KB)
         LAST_AT = 20 * KB
         ROUND_AT = 22 * KB
@@ -62,38 +61,38 @@ def tile_moe_wsel_b_silu_p_kernel(
         w2s_all = keep.tile([P, E * N], U8, align_bytes=64)
         x_plane = keep.tile([P, T], U8, align_bytes=64)
         w1_all = keep.tile([P, E * H], I32, align_bytes=64)
-        zeros = at(GATE_AT - 64, [P, P + 32], F32, "zeros")
+        zeros = at(W2_AT - 256, [P, P], F32, "zeros")
+        gate_rows = keep.tile([P, P], F32, align_bytes=64)
         ident = keep.tile([P, P], F32)
-        zero_col = keep.tile([P, 1], F32, align_bytes=64)
+        zero_col = keep.tile([P, 1], F32, align_bytes=64, tag="gate_cols")
         biases = {
             0: keep.tile([P, 1], F32, align_bytes=64, name="bias0"),
             3: at(DEALT_AT[0], [P, 1], F32, "bias3"),
-            6: at(DEALT_AT[1], [P, 1], F32, "bias6"),
+            7: at(DEALT_AT[1], [P, 1], F32, "bias7"),
         }
 
-        nc.gpsimd.memset(w1s_all[:, 0:E * H // 2].bitcast(I32), 0)
         nc.gpsimd.memset(w1_all[:, EARLY:EARLY + P], 0)
+        nc.gpsimd.memset(w1s_all[:, 0:E * H // 2].bitcast(I32), 0)
         nc.gpsimd.memset(zero_col[:], 0.0)
-        nc.gpsimd.memset(w2s_all[:].bitcast(I32), 0)
-        nc.gpsimd.memset(biases[3][:], 0.0)
-        nc.gpsimd.memset(biases[6][:], 0.0)
-        nc.scalar.activation(out=biases[0][:, 0:1], in_=zero_col[:], func=SILU)
-        nc.vector.memset(w1s_all[:, E * H // 2:E * H].bitcast(I32), 0)
-        nc.vector.tensor_copy(out=x_plane[:].bitcast(I32), in_=w1_all[:, EARLY:EARLY + P])
-        nc.vector.memset(zeros[:, 0:P], 0.0)
+        nc.gpsimd.memset(gate_rows[:], 0.0)
+        gate_runs = gate.rearrange("r q (c p) -> (r q c) p", p=P)
+        nc.gpsimd.dma_start(out=gate_rows[0:G * CHUNKS, :], in_=gate_runs[0:G * P * CHUNKS:P + 1, :])
+        nc.gpsimd.memset(zeros[:], 0.0)
         nc.gpsimd.affine_select(
             out=ident[:],
-            in_=zeros[:, 0:P],
+            in_=zeros[:],
             compare_op=mybir.AluOpType.not_equal,
             fill=1.0,
             base=0,
             pattern=[[-1, P]],
             channel_multiplier=1,
         )
-        gate_rows = at(GATE_AT, [P, P], F32, "gate_rows")
-        nc.gpsimd.memset(gate_rows[:], 0.0)
-        gate_runs = gate.rearrange("r q (c p) -> (r q c) p", p=P)
-        nc.gpsimd.dma_start(out=gate_rows[0:G * CHUNKS, :], in_=gate_runs[0:G * P * CHUNKS:P + 1, :])
+        nc.scalar.activation(out=biases[0][:], in_=zero_col[:], func=SILU)
+        nc.vector.memset(w1s_all[:, E * H // 2:E * H].bitcast(I32), 0)
+        nc.vector.tensor_copy(out=x_plane[:].bitcast(I32), in_=w1_all[:, EARLY:EARLY + P])
+        nc.vector.memset(w2s_all[:].bitcast(I32), 0)
+        nc.vector.memset(biases[3][:], 0.0)
+        nc.vector.memset(biases[7][:], 0.0)
 
         nc.sync.dma_start(list1[:], offs)
         nc.sync.dma_start(list2[:], offs2)
@@ -184,18 +183,17 @@ def tile_moe_wsel_b_silu_p_kernel(
             pick(w2_all[:].bitcast(U32), list2, r, dealt[:].bitcast(U32).rearrange("p (j m) -> p m j", j=PACK))
             return dealt
 
-        first_layer(0)
-        first_layer(1)
-        gate_bank = psum.tile([P, P], F32, tag="bank0")
+        gate_bank = psum.tile([P, P], F32, tag="bank7")
         nc.tensor.transpose(gate_bank[:], gate_rows[:], ident[:])
-        gate_cols = keep.tile([P, G * CHUNKS], F32, align_bytes=64)
+        gate_cols = keep.tile([P, G * CHUNKS], F32, align_bytes=64, tag="gate_cols")
         nc.scalar.copy(out=gate_cols[:], in_=gate_bank[:, 0:G * CHUNKS])
-        for k in range(2, 6):
+        for k in range(7):
             first_layer(k)
 
         w2s_picked = keep.tile([P, G * N], U8, align_bytes=64)
         nc.vector.tensor_copy(out=w2s_picked[:], in_=w2s_all[:].indirect(list2[:]))
-        apply_gate(0, False)
+        for k in range(2):
+            apply_gate(k, False)
         w2_plane = keep.tile([P, G * N], U8, align_bytes=64)
         nc.vector.tensor_copy(
             out=w2_plane[:].rearrange("p (r j b i) -> p r b j i", r=G, j=PACK, i=16),
@@ -203,15 +201,14 @@ def tile_moe_wsel_b_silu_p_kernel(
         )
         for q in range(1, 4):
             nc.sync.dma_start(out=w2_plane[q:P:32, :].bitcast(I32), in_=w2_plane[8 * q:P:32, :].bitcast(I32))
-        for k in range(1, 4):
+        for k in range(2, 4):
             apply_gate(k, False)
         w2_codes = [pick_dealt(0)]
         for k in range(4, 6):
             apply_gate(k, False)
 
         grouped = [turn(0)]
-        for k in range(6, 8):
-            first_layer(k)
+        first_layer(7)
         grouped.append(turn(1))
         h_codes = [keep.tile([P, HALF], I32, align_bytes=64, name="h_codes%d" % i) for i in range(2)]
         hq = [quantize_hidden(0, grouped[0], h_codes[0])]
@@ -247,9 +244,11 @@ def tile_moe_wsel_b_silu_p_kernel(
         def copy_out(half, sums, rows, j):
             engine = nc.scalar.copy if j < 2 + half else nc.vector.tensor_copy
             engine(out=rows[:, j, :], in_=sums[j][:])
-            if j % 2:
+            group = 2 * (half + 1)
+            if (j + 1) % group == 0:
+                first = j + 1 - group
                 nc.sync.dma_start(
-                    out=out_rows[:, j - 1:j + 1, half * HALF:(half + 1) * HALF], in_=rows[:, j - 1:j + 1, :]
+                    out=out_rows[:, first:j + 1, half * HALF:(half + 1) * HALF], in_=rows[:, first:j + 1, :]
                 )
 
         def round_and_group(engine, y_rows, out):

@@ -23,7 +23,8 @@ LIST_COLS = H // 16
 X_ROW = 8
 HALF = T // 2
 KB = 1024
-EARLY = 768
+W1_ROWS = 112
+W2_ROWS = 48
 
 
 def load_scale_rows(queues, plane, scales, first_row):
@@ -49,19 +50,22 @@ def tile_moe_wsel_b_silu_p_kernel(
         def at(offset, shape, dtype, name):
             return placed.tile(shape, dtype, align_bytes=64, offset=offset, name=name)
 
-        X_AT = 0
-        W2_AT = 2 * KB
-        DEALT_AT = (16 * KB, 18 * KB)
-        LAST_AT = 20 * KB
-        ROUND_AT = 22 * KB
+        W1S_AT = 0
+        W2_AT = 3 * KB - 64
+        SCALES_AT = 15 * KB
+        DEALT_AT = (18 * KB, 20 * KB)
+        LAST_AT = 22 * KB
+        ROUND_AT = 24 * KB
 
         list1 = keep.tile([P, G * LIST_COLS], U16)
         list2 = keep.tile([P, G * LIST_COLS], U16)
-        w1s_all = keep.tile([P, E * H], U8, align_bytes=64)
+        w1s_all = at(W1S_AT, [P, E * H], U8, "w1s_all")
         w2s_all = keep.tile([P, E * N], U8, align_bytes=64)
         x_plane = keep.tile([P, T], U8, align_bytes=64)
+        w1_plane = keep.tile([P, G * H], U8, align_bytes=64)
+        x_codes = keep.tile([P, T], I32, align_bytes=64)
         w1_all = keep.tile([P, E * H], I32, align_bytes=64)
-        zeros = at(W2_AT - 256, [P, P], F32, "zeros")
+        zeros = keep.tile([P, P], F32, align_bytes=64)
         gate_rows = keep.tile([P, P], F32, align_bytes=64)
         ident = keep.tile([P, P], F32)
         zero_col = keep.tile([P, 1], F32, align_bytes=64, tag="gate_cols")
@@ -71,8 +75,7 @@ def tile_moe_wsel_b_silu_p_kernel(
             7: at(DEALT_AT[1], [P, 1], F32, "bias7"),
         }
 
-        nc.gpsimd.memset(w1_all[:, EARLY:EARLY + P], 0)
-        nc.gpsimd.memset(w1s_all[:, 0:E * H // 2].bitcast(I32), 0)
+        nc.gpsimd.memset(x_plane[:].bitcast(I32), 0)
         nc.gpsimd.memset(zero_col[:], 0.0)
         nc.gpsimd.memset(gate_rows[:], 0.0)
         gate_runs = gate.rearrange("r q (c p) -> (r q c) p", p=P)
@@ -87,30 +90,39 @@ def tile_moe_wsel_b_silu_p_kernel(
             pattern=[[-1, P]],
             channel_multiplier=1,
         )
-        nc.scalar.activation(out=biases[0][:], in_=zero_col[:], func=SILU)
-        nc.vector.memset(w1s_all[:, E * H // 2:E * H].bitcast(I32), 0)
-        nc.vector.tensor_copy(out=x_plane[:].bitcast(I32), in_=w1_all[:, EARLY:EARLY + P])
-        nc.vector.memset(w2s_all[:].bitcast(I32), 0)
-        nc.vector.memset(biases[3][:], 0.0)
-        nc.vector.memset(biases[7][:], 0.0)
+        nc.gpsimd.memset(biases[3][:], 0.0)
+        nc.gpsimd.memset(biases[7][:], 0.0)
+        nc.vector.memset(w1s_all[0:W1_ROWS, :].bitcast(I32), 0)
+        nc.vector.memset(w2s_all[0:W2_ROWS, :].bitcast(I32), 0)
+        nc.vector.memset(w2s_all[W2_ROWS + 16:P, :].bitcast(I32), 0)
+        nc.vector.memset(w1_plane[:].bitcast(I32), 0)
 
         nc.sync.dma_start(list1[:], offs)
+        nc.sync.dma_start(out=w1s_all[W1_ROWS:W1_ROWS + 16, :].bitcast(I32), in_=w1_scales[0].bitcast(I32))
         nc.sync.dma_start(list2[:], offs2)
-        nc.sync.dma_start(out=w1_all[:, 0:EARLY], in_=words_of(w1_words)[:, 0:EARLY])
-        load_scale_rows([nc.sync], w1s_all, w1_scales, 0)
-        nc.sync.dma_start(out=w1_all[:, EARLY:E * H], in_=words_of(w1_words)[:, EARLY:E * H])
-        load_scale_rows([nc.sync], x_plane, x_scales, X_ROW)
-        x_codes = at(X_AT, [P, T], I32, "x_codes")
+        nc.sync.dma_start(out=w2s_all[W2_ROWS:W2_ROWS + 16, :].bitcast(I32), in_=w2_scales[0].bitcast(I32))
+        nc.sync.dma_start(out=w1_all[:], in_=words_of(w1_words))
         nc.sync.dma_start(out=x_codes[:], in_=words_of(x_words))
-        nc.sync.dma_start(out=w2s_all[0:P:8, :].bitcast(I32), in_=w2_scales[0].bitcast(I32))
-        w2_all = at(W2_AT, [P, E * N], I32, "w2_all")
-        nc.sync.dma_start(out=w2_all[:], in_=words_of(w2_words))
+        load_scale_rows([nc.scalar, nc.scalar, nc.scalar, nc.sync], x_plane, x_scales, X_ROW)
+        nc.scalar.activation(out=biases[0][:, 0:1], in_=zero_col[:], func=SILU)
+
+        def place_scale_rows(queues, plane, picked, first_row):
+            for q in range(4):
+                queues[q % len(queues)].dma_start(
+                    out=plane[32 * q:32 * q + 4, :].bitcast(I32),
+                    in_=picked[first_row + 4 * q:first_row + 4 * q + 4, :].bitcast(I32),
+                )
 
         def pick(window, offsets, r, out):
             nc.vector.tensor_copy(out=out, in_=window.indirect(offsets[:, r * LIST_COLS:(r + 1) * LIST_COLS]))
 
-        w1_plane = keep.tile([P, G * H], U8, align_bytes=64)
-        nc.vector.tensor_copy(out=w1_plane[:], in_=w1s_all[:].indirect(list1[:]))
+        w1s_picked = at(SCALES_AT, [P, G * H], U8, "w1s_picked")
+        nc.vector.tensor_copy(out=w1s_picked[:], in_=w1s_all[:].indirect(list1[:]))
+        place_scale_rows([nc.sync], w1_plane, w1s_picked, W1_ROWS)
+        w2_all = at(W2_AT, [P, E * N], I32, "w2_all")
+        nc.sync.dma_start(out=w2_all[:], in_=words_of(w2_words))
+        w2s_first = keep.tile([P, N], U8, align_bytes=64)
+        pick(w2s_all[:], list2, 0, w2s_first[:])
         w1_codes = []
         for r in range(G):
             picked = keep.tile([P, H], I32, align_bytes=64, name="w1_codes%d" % r)
@@ -178,6 +190,24 @@ def tile_moe_wsel_b_silu_p_kernel(
             nc.vector.quantize_mx(out=codes[:].bitcast(FP8X4), scales=plane[:], in_=grouped[:])
             return codes, plane
 
+        def deal_scales(r, picked):
+            nc.vector.tensor_copy(
+                out=w2_plane[:, r * N:(r + 1) * N].rearrange("p (j b i) -> p b j i", j=PACK, i=16),
+                in_=picked[:].rearrange("p (b i j) -> p b j i", j=PACK, i=16),
+            )
+
+        def keep_clock(bank):
+            unread = psum.tile([P, H], F32, tag="bank%d" % bank, name="unread%d" % bank)
+            nc.tensor.matmul_mx(
+                out=unread[:],
+                lhsT=x_codes[:, 0:P].bitcast(FP8X4),
+                lhsT_scale=x_plane[X_ROW:P, 0:P],
+                rhs=w1_codes[0][:].bitcast(FP8X4),
+                rhs_scale=w1_plane[:, 0:H],
+                start=True,
+                stop=True,
+            )
+
         def pick_dealt(r):
             dealt = at(DEALT_AT[r], [P, N], I32, "w2_codes%d" % r)
             pick(w2_all[:].bitcast(U32), list2, r, dealt[:].bitcast(U32).rearrange("p (j m) -> p m j", j=PACK))
@@ -190,17 +220,14 @@ def tile_moe_wsel_b_silu_p_kernel(
         for k in range(7):
             first_layer(k)
 
-        w2s_picked = keep.tile([P, G * N], U8, align_bytes=64)
-        nc.vector.tensor_copy(out=w2s_picked[:], in_=w2s_all[:].indirect(list2[:]))
+        w2s_second = at(SCALES_AT, [P, N], U8, "w2s_second")
+        pick(w2s_all[:], list2, 1, w2s_second[:])
+        w2_plane = at(SCALES_AT + 512, [P, G * N], U8, "w2_plane")
+        deal_scales(0, w2s_first)
         for k in range(2):
             apply_gate(k, False)
-        w2_plane = keep.tile([P, G * N], U8, align_bytes=64)
-        nc.vector.tensor_copy(
-            out=w2_plane[:].rearrange("p (r j b i) -> p r b j i", r=G, j=PACK, i=16),
-            in_=w2s_picked[:].rearrange("p (r b i j) -> p r b j i", r=G, j=PACK, i=16),
-        )
-        for q in range(1, 4):
-            nc.sync.dma_start(out=w2_plane[q:P:32, :].bitcast(I32), in_=w2_plane[8 * q:P:32, :].bitcast(I32))
+        deal_scales(1, w2s_second)
+        place_scale_rows([nc.sync], w2_plane, w2_plane, W2_ROWS)
         for k in range(2, 4):
             apply_gate(k, False)
         w2_codes = [pick_dealt(0)]
@@ -210,6 +237,8 @@ def tile_moe_wsel_b_silu_p_kernel(
         grouped = [turn(0)]
         first_layer(7)
         grouped.append(turn(1))
+        for bank in (6, 0, 7):
+            keep_clock(bank)
         h_codes = [keep.tile([P, HALF], I32, align_bytes=64, name="h_codes%d" % i) for i in range(2)]
         hq = [quantize_hidden(0, grouped[0], h_codes[0])]
         gated.append(at(LAST_AT, [P, 2 * H], BF16, "gated3"))

@@ -273,9 +273,8 @@ def tile_moe_wsel_b_silu_p_kernel(
         def copy_out(half, sums, rows, j):
             engine = nc.scalar.copy if j < 2 + half else nc.vector.tensor_copy
             engine(out=rows[:, j, :], in_=sums[j][:])
-            group = 2 * (half + 1)
-            if (j + 1) % group == 0:
-                first = j + 1 - group
+            first = j if half == 0 and j < 2 else j - 1
+            if first == j or j % 2:
                 nc.sync.dma_start(
                     out=out_rows[:, first:j + 1, half * HALF:(half + 1) * HALF], in_=rows[:, first:j + 1, :]
                 )

@@ -18,20 +18,28 @@ MULT = mybir.AluOpType.mult
 
 P = 128
 PACK = 4
+QUADRANTS = 4
+BLOCKS = 16
 CHUNKS = T // P
-LIST_COLS = H // 16
-X_ROW = 8
 HALF = T // 2
+LIST_COLS = H // 16
 KB = 1024
+
+X_ROW = 8
 W1_ROWS = 112
 W2_ROWS = 48
+EARLY = 2048
 
+W1S_AT = 0
+W2_AT = 3 * KB - 64
+SCALES_AT = 15 * KB
+DEALT_AT = (18 * KB, 20 * KB)
+LAST_AT = 22 * KB
+ROUND_AT = 24 * KB
+GATES_AT = 26 * KB
 
-def load_scale_rows(queues, plane, scales, first_row):
-    for q in range(4):
-        queues[q % len(queues)].dma_start(
-            out=plane[first_row + q:P:32, :].bitcast(I32), in_=scales[0, q:16:4, :].bitcast(I32)
-        )
+HOLDING_UNITS = (3, 7)
+SCALAR_UNIT = 6
 
 
 def words_of(packed):
@@ -50,33 +58,23 @@ def tile_moe_wsel_b_silu_p_kernel(
         def at(offset, shape, dtype, name):
             return placed.tile(shape, dtype, align_bytes=64, offset=offset, name=name)
 
-        W1S_AT = 0
-        W2_AT = 3 * KB - 64
-        SCALES_AT = 15 * KB
-        DEALT_AT = (18 * KB, 20 * KB)
-        LAST_AT = 22 * KB
-        ROUND_AT = 24 * KB
-
         list1 = keep.tile([P, G * LIST_COLS], U16)
         list2 = keep.tile([P, G * LIST_COLS], U16)
         w1s_all = at(W1S_AT, [P, E * H], U8, "w1s_all")
         w2s_all = keep.tile([P, E * N], U8, align_bytes=64)
         x_plane = keep.tile([P, T], U8, align_bytes=64)
         w1_plane = keep.tile([P, G * H], U8, align_bytes=64)
-        x_codes = keep.tile([P, T], I32, align_bytes=64)
         w1_all = keep.tile([P, E * H], I32, align_bytes=64)
         zeros = keep.tile([P, P], F32, align_bytes=64)
         gate_rows = keep.tile([P, P], F32, align_bytes=64)
         ident = keep.tile([P, P], F32)
-        zero_col = keep.tile([P, 1], F32, align_bytes=64, tag="gate_cols")
-        biases = {
-            0: keep.tile([P, 1], F32, align_bytes=64, name="bias0"),
-            3: at(DEALT_AT[0], [P, 1], F32, "bias3"),
-            7: at(DEALT_AT[1], [P, 1], F32, "bias7"),
-        }
+        zero_col = at(GATES_AT, [P, 32], F32, "zero_col")
+        biases = {0: keep.tile([P, 1], F32, align_bytes=64, name="bias0")}
+        for r, k in enumerate(HOLDING_UNITS):
+            biases[k] = at(DEALT_AT[r], [P, 1], F32, "bias%d" % k)
 
-        nc.gpsimd.memset(x_plane[:].bitcast(I32), 0)
-        nc.gpsimd.memset(zero_col[:], 0.0)
+        nc.gpsimd.memset(w1_all[:, EARLY:EARLY + P], 0)
+        nc.gpsimd.memset(zero_col[:, 0:1], 0.0)
         nc.gpsimd.memset(gate_rows[:], 0.0)
         gate_runs = gate.rearrange("r q (c p) -> (r q c) p", p=P)
         nc.gpsimd.dma_start(out=gate_rows[0:G * CHUNKS, :], in_=gate_runs[0:G * P * CHUNKS:P + 1, :])
@@ -90,27 +88,31 @@ def tile_moe_wsel_b_silu_p_kernel(
             pattern=[[-1, P]],
             channel_multiplier=1,
         )
-        nc.gpsimd.memset(biases[3][:], 0.0)
-        nc.gpsimd.memset(biases[7][:], 0.0)
+        for k in HOLDING_UNITS:
+            nc.gpsimd.memset(biases[k][:], 0.0)
+        nc.vector.tensor_copy(out=x_plane[:].bitcast(I32), in_=w1_all[:, EARLY:EARLY + P])
         nc.vector.memset(w1s_all[0:W1_ROWS, :].bitcast(I32), 0)
         nc.vector.memset(w2s_all[0:W2_ROWS, :].bitcast(I32), 0)
-        nc.vector.memset(w2s_all[W2_ROWS + 16:P, :].bitcast(I32), 0)
+        nc.vector.memset(w2s_all[W2_ROWS + BLOCKS:P, :].bitcast(I32), 0)
         nc.vector.memset(w1_plane[:].bitcast(I32), 0)
 
         nc.sync.dma_start(list1[:], offs)
-        nc.sync.dma_start(out=w1s_all[W1_ROWS:W1_ROWS + 16, :].bitcast(I32), in_=w1_scales[0].bitcast(I32))
+        nc.sync.dma_start(out=w1s_all[W1_ROWS:W1_ROWS + BLOCKS, :].bitcast(I32), in_=w1_scales[0].bitcast(I32))
         nc.sync.dma_start(list2[:], offs2)
-        nc.sync.dma_start(out=w2s_all[W2_ROWS:W2_ROWS + 16, :].bitcast(I32), in_=w2_scales[0].bitcast(I32))
-        nc.sync.dma_start(out=w1_all[:], in_=words_of(w1_words))
+        nc.sync.dma_start(out=w2s_all[W2_ROWS:W2_ROWS + BLOCKS, :].bitcast(I32), in_=w2_scales[0].bitcast(I32))
+        nc.sync.dma_start(out=w1_all[:, 0:EARLY], in_=words_of(w1_words)[:, 0:EARLY])
+        for i in range(PACK):
+            nc.sync.dma_start(out=x_plane[X_ROW + i:P:32, :].bitcast(I32), in_=x_scales[0, i:BLOCKS:4, :].bitcast(I32))
+        nc.sync.dma_start(out=w1_all[:, EARLY:E * H], in_=words_of(w1_words)[:, EARLY:E * H])
+        x_codes = at(GATES_AT + 64, [P, T], I32, "x_codes")
         nc.sync.dma_start(out=x_codes[:], in_=words_of(x_words))
-        load_scale_rows([nc.scalar, nc.scalar, nc.scalar, nc.sync], x_plane, x_scales, X_ROW)
-        nc.scalar.activation(out=biases[0][:, 0:1], in_=zero_col[:], func=SILU)
+        nc.scalar.activation(out=biases[0][:, 0:1], in_=zero_col[:, 0:1], func=SILU)
 
-        def place_scale_rows(queues, plane, picked, first_row):
-            for q in range(4):
-                queues[q % len(queues)].dma_start(
+        def place_scale_rows(plane, rows, first_row):
+            for q in range(QUADRANTS):
+                nc.sync.dma_start(
                     out=plane[32 * q:32 * q + 4, :].bitcast(I32),
-                    in_=picked[first_row + 4 * q:first_row + 4 * q + 4, :].bitcast(I32),
+                    in_=rows[first_row + 4 * q:first_row + 4 * q + 4, :].bitcast(I32),
                 )
 
         def pick(window, offsets, r, out):
@@ -118,7 +120,7 @@ def tile_moe_wsel_b_silu_p_kernel(
 
         w1s_picked = at(SCALES_AT, [P, G * H], U8, "w1s_picked")
         nc.vector.tensor_copy(out=w1s_picked[:], in_=w1s_all[:].indirect(list1[:]))
-        place_scale_rows([nc.sync], w1_plane, w1s_picked, W1_ROWS)
+        place_scale_rows(w1_plane, w1s_picked, W1_ROWS)
         w2_all = at(W2_AT, [P, E * N], I32, "w2_all")
         nc.sync.dma_start(out=w2_all[:], in_=words_of(w2_words))
         w2s_first = keep.tile([P, N], U8, align_bytes=64)
@@ -161,11 +163,11 @@ def tile_moe_wsel_b_silu_p_kernel(
 
         gated = [keep.tile([P, 2 * H], BF16, align_bytes=64, name="gated%d" % i) for i in range(3)]
 
-        def apply_gate(k, on_scalar):
+        def apply_gate(k):
             half, r, cc = units[k]
             col = r * CHUNKS + 2 * half + cc
             h_tok = gated[k // 2][:, cc * H:(cc + 1) * H]
-            if on_scalar:
+            if k == SCALAR_UNIT:
                 nc.scalar.activation(out=h_tok, in_=acts[k][:], func=COPY, scale=gate_cols[:, col:col + 1])
             else:
                 nc.vector.tensor_scalar(
@@ -174,10 +176,10 @@ def tile_moe_wsel_b_silu_p_kernel(
 
         def turn(i):
             turned = psum.tile([P, 2, 2, P], F32, tag="bank%d" % i)
-            pairs = gated[i][:].bitcast(F32)
+            words = gated[i][:].bitcast(F32)
             for cc in range(2):
                 for u in range(2):
-                    nc.tensor.transpose(turned[:, cc, u, :], pairs[:, (2 * cc + u) * P:(2 * cc + u + 1) * P], ident[:])
+                    nc.tensor.transpose(turned[:, cc, u, :], words[:, (2 * cc + u) * P:(2 * cc + u + 1) * P], ident[:])
             grouped = keep.tile([P, 2 * P * PACK], BF16, align_bytes=64, name="h_grouped%d" % i)
             nc.scalar.copy(
                 out=grouped[:].bitcast(F32).rearrange("p (c t u) -> p c t u", c=2, u=2),
@@ -215,36 +217,37 @@ def tile_moe_wsel_b_silu_p_kernel(
 
         gate_bank = psum.tile([P, P], F32, tag="bank7")
         nc.tensor.transpose(gate_bank[:], gate_rows[:], ident[:])
-        gate_cols = keep.tile([P, G * CHUNKS], F32, align_bytes=64, tag="gate_cols")
+        gate_cols = at(GATES_AT, [P, G * CHUNKS], F32, "gate_cols")
         nc.scalar.copy(out=gate_cols[:], in_=gate_bank[:, 0:G * CHUNKS])
-        for k in range(7):
+        last_unit = len(units) - 1
+        for k in range(last_unit):
             first_layer(k)
 
         w2s_second = at(SCALES_AT, [P, N], U8, "w2s_second")
         pick(w2s_all[:], list2, 1, w2s_second[:])
-        w2_plane = at(SCALES_AT + 512, [P, G * N], U8, "w2_plane")
+        w2_plane = at(SCALES_AT + N, [P, G * N], U8, "w2_plane")
         deal_scales(0, w2s_first)
         for k in range(2):
-            apply_gate(k, False)
+            apply_gate(k)
         deal_scales(1, w2s_second)
-        place_scale_rows([nc.sync], w2_plane, w2_plane, W2_ROWS)
+        place_scale_rows(w2_plane, w2_plane, W2_ROWS)
         for k in range(2, 4):
-            apply_gate(k, False)
+            apply_gate(k)
         w2_codes = [pick_dealt(0)]
         for k in range(4, 6):
-            apply_gate(k, False)
+            apply_gate(k)
 
         grouped = [turn(0)]
-        first_layer(7)
+        first_layer(last_unit)
+        gated.append(at(LAST_AT, [P, 2 * H], BF16, "gated3"))
+        apply_gate(SCALAR_UNIT)
         grouped.append(turn(1))
-        for bank in (6, 0, 7):
+        for bank in (last_unit - 1, 0, last_unit):
             keep_clock(bank)
         h_codes = [keep.tile([P, HALF], I32, align_bytes=64, name="h_codes%d" % i) for i in range(2)]
         hq = [quantize_hidden(0, grouped[0], h_codes[0])]
-        gated.append(at(LAST_AT, [P, 2 * H], BF16, "gated3"))
-        apply_gate(6, False)
+        apply_gate(last_unit)
         w2_codes.append(pick_dealt(1))
-        apply_gate(7, True)
         grouped.append(turn(2))
         grouped.append(turn(3))
         hq.append(quantize_hidden(1, grouped[1], at(LAST_AT, [P, HALF], I32, "h_codes_held")))
@@ -285,27 +288,26 @@ def tile_moe_wsel_b_silu_p_kernel(
                 in_=y_rows.rearrange("p j (b i) -> p b j i", i=4),
             )
 
-        def quantize_result(half, rounded):
+        def quantize_result(half, values):
             tokens = slice(half * HALF, (half + 1) * HALF)
-            nc.vector.quantize_mx(out=y_codes[:, tokens].bitcast(FP8X4), scales=y_plane[:, tokens], in_=rounded[:])
+            nc.vector.quantize_mx(out=y_codes[:, tokens].bitcast(FP8X4), scales=y_plane[:, tokens], in_=values[:])
             nc.sync.dma_start(out=out_words[:, tokens], in_=y_codes[:, tokens])
 
-        sums = [second_layer(0, 4), second_layer(1, 0)]
+        sums = [second_layer(0, PACK), second_layer(1, 0)]
         y = [keep.tile([P, PACK, HALF], F32, align_bytes=64, name="y%d" % half) for half in range(2)]
         rounded = [
             at(ROUND_AT, [P, PACK * HALF], BF16, "rounded0"),
             keep.tile([P, PACK * HALF], BF16, align_bytes=64, name="rounded1"),
         ]
-        for j in range(PACK):
-            copy_out(0, sums[0], y[0], j)
-        for j in range(PACK):
-            copy_out(1, sums[1], y[1], j)
+        for half in range(2):
+            for j in range(PACK):
+                copy_out(half, sums[half], y[half], j)
         round_and_group(nc.vector.tensor_copy, y[0][:], rounded[0][:])
         round_and_group(nc.vector.tensor_copy, y[1][:, :, 0:P], rounded[1][:, 0:PACK * P])
         round_and_group(nc.scalar.copy, y[1][:, :, P:HALF], rounded[1][:, PACK * P:PACK * HALF])
-        quantize_result(0, rounded[0])
-        quantize_result(1, rounded[1])
+        for half in range(2):
+            quantize_result(half, rounded[half])
 
-        for q in range(4):
-            queue = nc.scalar if q % 2 else nc.sync
-            queue.dma_start(out=out_2[0, q:16:4, :].bitcast(I32), in_=y_plane[q:P:32, :].bitcast(I32))
+        for i in range(PACK):
+            queue = nc.scalar if i % 2 else nc.sync
+            queue.dma_start(out=out_2[0, i:BLOCKS:4, :].bitcast(I32), in_=y_plane[i:P:32, :].bitcast(I32))

@@ -31,6 +31,7 @@ W2_ROWS = 48
 EARLY = 2048
 
 W1S_AT = 0
+X_LATE_AT = 2 * KB - 64
 W2_AT = 3 * KB - 64
 SCALES_AT = 15 * KB
 DEALT_AT = (18 * KB, 20 * KB)
@@ -104,13 +105,13 @@ def tile_moe_wsel_b_silu_p_kernel(
         for i in range(PACK):
             nc.sync.dma_start(out=x_plane[X_ROW + i:P:32, :].bitcast(I32), in_=x_scales[0, i:BLOCKS:4, :].bitcast(I32))
         nc.sync.dma_start(out=w1_all[:, EARLY:E * H], in_=words_of(w1_words)[:, EARLY:E * H])
-        x_codes = at(GATES_AT + 64, [P, T], I32, "x_codes")
-        nc.sync.dma_start(out=x_codes[:], in_=words_of(x_words))
+        x_codes = [at(GATES_AT + 64, [P, HALF], I32, "x_early")]
+        nc.sync.dma_start(out=x_codes[0][:], in_=words_of(x_words)[:, 0:HALF])
         nc.scalar.activation(out=biases[0][:, 0:1], in_=zero_col[:, 0:1], func=SILU)
 
-        def place_scale_rows(plane, rows, first_row):
+        def place_scale_rows(queue, plane, rows, first_row):
             for q in range(QUADRANTS):
-                nc.sync.dma_start(
+                queue.dma_start(
                     out=plane[32 * q:32 * q + 4, :].bitcast(I32),
                     in_=rows[first_row + 4 * q:first_row + 4 * q + 4, :].bitcast(I32),
                 )
@@ -120,7 +121,9 @@ def tile_moe_wsel_b_silu_p_kernel(
 
         w1s_picked = at(SCALES_AT, [P, G * H], U8, "w1s_picked")
         nc.vector.tensor_copy(out=w1s_picked[:], in_=w1s_all[:].indirect(list1[:]))
-        place_scale_rows(w1_plane, w1s_picked, W1_ROWS)
+        place_scale_rows(nc.sync, w1_plane, w1s_picked, W1_ROWS)
+        x_codes.append(at(X_LATE_AT, [P, HALF], I32, "x_late"))
+        nc.sync.dma_start(out=x_codes[1][:], in_=words_of(x_words)[:, HALF:T])
         w2_all = at(W2_AT, [P, E * N], I32, "w2_all")
         nc.sync.dma_start(out=w2_all[:], in_=words_of(w2_words))
         w2s_first = keep.tile([P, N], U8, align_bytes=64)
@@ -128,7 +131,13 @@ def tile_moe_wsel_b_silu_p_kernel(
         w1_codes = []
         for r in range(G):
             picked = keep.tile([P, H], I32, align_bytes=64, name="w1_codes%d" % r)
-            pick(w1_all[:].bitcast(U32), list1, r, picked[:].bitcast(U32))
+            parts = 2 if r == 0 else 1
+            for part in range(parts):
+                entries = slice((r * parts + part) * LIST_COLS // parts, (r * parts + part + 1) * LIST_COLS // parts)
+                nc.vector.tensor_copy(
+                    out=picked[:, part * H // parts:(part + 1) * H // parts].bitcast(U32),
+                    in_=w1_all[:].bitcast(U32).indirect(list1[:, entries]),
+                )
             w1_codes.append(picked)
 
         y_codes = keep.tile([P, T], I32, align_bytes=64)
@@ -139,27 +148,29 @@ def tile_moe_wsel_b_silu_p_kernel(
         units = [(half, r, cc) for half in range(2) for r in range(G) for cc in range(2)]
         acts = {}
 
-        def first_layer(k):
+        def first_layer(k, bank, hidden):
             half, r, cc = units[k]
             tokens = slice((2 * half + cc) * P, (2 * half + cc + 1) * P)
-            pre = psum.tile([P, H], F32, tag="bank%d" % k)
+            width = hidden.stop - hidden.start
+            pre = psum.tile([P, H], F32, tag="bank%d" % bank)
             nc.tensor.matmul_mx(
-                out=pre[:],
-                lhsT=x_codes[:, tokens].bitcast(FP8X4),
+                out=pre[:, 0:width],
+                lhsT=x_codes[half][:, cc * P:(cc + 1) * P].bitcast(FP8X4),
                 lhsT_scale=x_plane[X_ROW:P, tokens],
-                rhs=w1_codes[r][:].bitcast(FP8X4),
-                rhs_scale=w1_plane[:, r * H:(r + 1) * H],
+                rhs=w1_codes[r][:, hidden].bitcast(FP8X4),
+                rhs_scale=w1_plane[:, r * H + hidden.start:r * H + hidden.stop],
                 start=True,
                 stop=True,
             )
-            act = keep.tile([P, H], F32, align_bytes=64, name="act%d" % k)
+            if k not in acts:
+                acts[k] = keep.tile([P, H], F32, align_bytes=64, name="act%d" % k)
+            words = slice(hidden.start // PACK, hidden.stop // PACK)
             nc.scalar.activation(
-                out=act[:].rearrange("p (u m e) -> p u m e", u=2, e=2),
-                in_=pre[:].rearrange("p (m u e) -> p u m e", u=2, e=2),
+                out=acts[k][:].rearrange("p (u m e) -> p u m e", u=2, e=2)[:, :, words, :],
+                in_=pre[:, 0:width].rearrange("p (m u e) -> p u m e", u=2, e=2),
                 func=SILU,
                 bias=biases[k][:, 0:1] if k in biases else 0.0,
             )
-            acts[k] = act
 
         gated = [keep.tile([P, 2 * H], BF16, align_bytes=64, name="gated%d" % i) for i in range(3)]
 
@@ -202,7 +213,7 @@ def tile_moe_wsel_b_silu_p_kernel(
             unread = psum.tile([P, H], F32, tag="bank%d" % bank, name="unread%d" % bank)
             nc.tensor.matmul_mx(
                 out=unread[:],
-                lhsT=x_codes[:, 0:P].bitcast(FP8X4),
+                lhsT=x_codes[0][:, 0:P].bitcast(FP8X4),
                 lhsT_scale=x_plane[X_ROW:P, 0:P],
                 rhs=w1_codes[0][:].bitcast(FP8X4),
                 rhs_scale=w1_plane[:, 0:H],
@@ -215,22 +226,26 @@ def tile_moe_wsel_b_silu_p_kernel(
             pick(w2_all[:].bitcast(U32), list2, r, dealt[:].bitcast(U32).rearrange("p (j m) -> p m j", j=PACK))
             return dealt
 
-        gate_bank = psum.tile([P, P], F32, tag="bank7")
+        gate_bank = psum.tile([P, P], F32, tag="bank5")
         nc.tensor.transpose(gate_bank[:], gate_rows[:], ident[:])
         gate_cols = at(GATES_AT, [P, G * CHUNKS], F32, "gate_cols")
         nc.scalar.copy(out=gate_cols[:], in_=gate_bank[:, 0:G * CHUNKS])
         last_unit = len(units) - 1
-        for k in range(last_unit):
-            first_layer(k)
+        whole = slice(0, H)
+        for part in range(2):
+            for k in range(2):
+                first_layer(k, (k + 6 * (1 - part)) % 8, slice(part * H // 2, (part + 1) * H // 2))
+        for k in range(2, last_unit):
+            first_layer(k, k, whole)
 
-        w2s_second = at(SCALES_AT, [P, N], U8, "w2s_second")
+        w2s_second = at(SCALES_AT + 64, [P, N], U8, "w2s_second")
         pick(w2s_all[:], list2, 1, w2s_second[:])
-        w2_plane = at(SCALES_AT + N, [P, G * N], U8, "w2_plane")
+        w2_plane = at(SCALES_AT + 64 + N, [P, G * N], U8, "w2_plane")
         deal_scales(0, w2s_first)
         for k in range(2):
             apply_gate(k)
         deal_scales(1, w2s_second)
-        place_scale_rows(w2_plane, w2_plane, W2_ROWS)
+        place_scale_rows(nc.sync, w2_plane, w2_plane, W2_ROWS)
         for k in range(2, 4):
             apply_gate(k)
         w2_codes = [pick_dealt(0)]
@@ -238,7 +253,7 @@ def tile_moe_wsel_b_silu_p_kernel(
             apply_gate(k)
 
         grouped = [turn(0)]
-        first_layer(last_unit)
+        first_layer(last_unit, last_unit, whole)
         gated.append(at(LAST_AT, [P, 2 * H], BF16, "gated3"))
         apply_gate(SCALAR_UNIT)
         grouped.append(turn(1))

@@ -41,6 +41,10 @@ GATES_AT = 26 * KB
 
 HOLDING_UNITS = (3, 7)
 SCALAR_UNIT = 6
+UNIT_BANKS = (0, 1, 2, 3, 4, 2, 3, 2)
+TURN_BANKS = (0, 1, 4, 3)
+SUM_BANKS = ((6, 7, 5, 0), (1, 4, 2, 3))
+VECTOR_ROUNDS = 160
 
 
 def words_of(packed):
@@ -172,7 +176,7 @@ def tile_moe_wsel_b_silu_p_kernel(
                 bias=biases[k][:, 0:1] if k in biases else 0.0,
             )
 
-        gated = [keep.tile([P, 2 * H], BF16, align_bytes=64, name="gated%d" % i) for i in range(3)]
+        gated = [keep.tile([P, 2 * H], BF16, align_bytes=64, name="gated%d" % i) for i in range(4)]
 
         def apply_gate(k):
             half, r, cc = units[k]
@@ -186,7 +190,7 @@ def tile_moe_wsel_b_silu_p_kernel(
                 )
 
         def turn(i):
-            turned = psum.tile([P, 2, 2, P], F32, tag="bank%d" % i)
+            turned = psum.tile([P, 2, 2, P], F32, tag="bank%d" % TURN_BANKS[i])
             words = gated[i][:].bitcast(F32)
             for cc in range(2):
                 for u in range(2):
@@ -209,14 +213,14 @@ def tile_moe_wsel_b_silu_p_kernel(
                 in_=picked[:].rearrange("p (b i j) -> p b j i", j=PACK, i=16),
             )
 
-        def keep_clock(bank):
-            unread = psum.tile([P, H], F32, tag="bank%d" % bank, name="unread%d" % bank)
+        def keep_clock(bank, width):
+            unread = psum.tile([P, width], F32, tag="bank%d" % bank, name="unread%d" % bank)
             nc.tensor.matmul_mx(
                 out=unread[:],
                 lhsT=x_codes[0][:, 0:P].bitcast(FP8X4),
                 lhsT_scale=x_plane[X_ROW:P, 0:P],
-                rhs=w1_codes[0][:].bitcast(FP8X4),
-                rhs_scale=w1_plane[:, 0:H],
+                rhs=w1_codes[0][:, 0:width].bitcast(FP8X4),
+                rhs_scale=w1_plane[:, 0:width],
                 start=True,
                 stop=True,
             )
@@ -230,13 +234,12 @@ def tile_moe_wsel_b_silu_p_kernel(
         nc.tensor.transpose(gate_bank[:], gate_rows[:], ident[:])
         gate_cols = at(GATES_AT, [P, G * CHUNKS], F32, "gate_cols")
         nc.scalar.copy(out=gate_cols[:], in_=gate_bank[:, 0:G * CHUNKS])
-        last_unit = len(units) - 1
         whole = slice(0, H)
         for part in range(2):
             for k in range(2):
                 first_layer(k, (k + 6 * (1 - part)) % 8, slice(part * H // 2, (part + 1) * H // 2))
-        for k in range(2, last_unit):
-            first_layer(k, k, whole)
+        for k in range(2, 7):
+            first_layer(k, UNIT_BANKS[k], whole)
 
         w2s_second = at(SCALES_AT + 64, [P, N], U8, "w2s_second")
         pick(w2s_all[:], list2, 1, w2s_second[:])
@@ -253,25 +256,23 @@ def tile_moe_wsel_b_silu_p_kernel(
             apply_gate(k)
 
         grouped = [turn(0)]
-        first_layer(last_unit, last_unit, whole)
-        gated.append(at(LAST_AT, [P, 2 * H], BF16, "gated3"))
-        apply_gate(SCALAR_UNIT)
+        first_layer(7, UNIT_BANKS[7], whole)
+        apply_gate(6)
         grouped.append(turn(1))
-        for bank in (last_unit - 1, 0, last_unit):
-            keep_clock(bank)
-        h_codes = [keep.tile([P, HALF], I32, align_bytes=64, name="h_codes%d" % i) for i in range(2)]
+        keep_clock(TURN_BANKS[0], H)
+        keep_clock(UNIT_BANKS[7], H // 2)
+        h_codes = [keep.tile([P, HALF], I32, align_bytes=64, name="h_codes%d" % i) for i in range(4)]
         hq = [quantize_hidden(0, grouped[0], h_codes[0])]
-        apply_gate(last_unit)
+        apply_gate(7)
         w2_codes.append(pick_dealt(1))
-        grouped.append(turn(2))
-        grouped.append(turn(3))
-        hq.append(quantize_hidden(1, grouped[1], at(LAST_AT, [P, HALF], I32, "h_codes_held")))
-        hq.append(quantize_hidden(2, grouped[2], h_codes[1]))
-        hq.append(quantize_hidden(3, grouped[3], at(ROUND_AT, [P, HALF], I32, "h_codes_last")))
+        for i in range(2, 4):
+            grouped.append(turn(i))
+        for i in range(1, 4):
+            hq.append(quantize_hidden(i, grouped[i], h_codes[i]))
 
-        def second_layer(half, first_bank):
+        def second_layer(half):
             sums = [
-                psum.tile([P, HALF], F32, tag="bank%d" % (first_bank + j), name="sums%d%d" % (half, j))
+                psum.tile([P, HALF], F32, tag="bank%d" % SUM_BANKS[half][j], name="sums%d%d" % (half, j))
                 for j in range(PACK)
             ]
             for r in range(G):
@@ -308,20 +309,18 @@ def tile_moe_wsel_b_silu_p_kernel(
             nc.vector.quantize_mx(out=y_codes[:, tokens].bitcast(FP8X4), scales=y_plane[:, tokens], in_=values[:])
             nc.sync.dma_start(out=out_words[:, tokens], in_=y_codes[:, tokens])
 
-        sums = [second_layer(0, PACK), second_layer(1, 0)]
+        sums = [second_layer(half) for half in range(2)]
         y = [keep.tile([P, PACK, HALF], F32, align_bytes=64, name="y%d" % half) for half in range(2)]
-        rounded = [
-            at(ROUND_AT, [P, PACK * HALF], BF16, "rounded0"),
-            keep.tile([P, PACK * HALF], BF16, align_bytes=64, name="rounded1"),
-        ]
-        for half in range(2):
-            for j in range(PACK):
-                copy_out(half, sums[half], y[half], j)
+        rounded = [keep.tile([P, PACK * HALF], BF16, align_bytes=64, name="rounded%d" % half) for half in range(2)]
+        for j in range(PACK):
+            copy_out(0, sums[0], y[0], j)
         round_and_group(nc.vector.tensor_copy, y[0][:], rounded[0][:])
-        round_and_group(nc.vector.tensor_copy, y[1][:, :, 0:P], rounded[1][:, 0:PACK * P])
-        round_and_group(nc.scalar.copy, y[1][:, :, P:HALF], rounded[1][:, PACK * P:PACK * HALF])
-        for half in range(2):
-            quantize_result(half, rounded[half])
+        for j in range(PACK):
+            copy_out(1, sums[1], y[1], j)
+        quantize_result(0, rounded[0])
+        round_and_group(nc.vector.tensor_copy, y[1][:, :, 0:VECTOR_ROUNDS], rounded[1][:, 0:PACK * VECTOR_ROUNDS])
+        round_and_group(nc.scalar.copy, y[1][:, :, VECTOR_ROUNDS:HALF], rounded[1][:, PACK * VECTOR_ROUNDS:PACK * HALF])
+        quantize_result(1, rounded[1])
 
         for i in range(PACK):
             queue = nc.scalar if i % 2 else nc.sync

@@ -42,8 +42,8 @@ GATES_AT = 26 * KB
 HOLDING_UNITS = (3, 7)
 SCALAR_UNIT = 6
 UNIT_BANKS = (0, 1, 2, 3, 4, 2, 3, 2)
-TURN_BANKS = (0, 1, 4, 3)
-SUM_BANKS = ((6, 7, 5, 0), (1, 4, 2, 3))
+TURN_BANKS = (4, 3, 0, 1)
+SUM_BANKS = ((6, 7, 5, 4), (3, 0, 2, 1))
 VECTOR_ROUNDS = 160
 
 

@@ -15,6 +15,7 @@ FP8X4 = mybir.dt.float8_e4m3fn_x4
 SILU = mybir.ActivationFunctionType.Silu
 COPY = mybir.ActivationFunctionType.Copy
 MULT = mybir.AluOpType.mult
+ADD = mybir.AluOpType.add
 
 P = 128
 PACK = 4
@@ -37,10 +38,12 @@ SCALES_AT = 15 * KB
 DEALT_AT = (18 * KB, 20 * KB)
 LAST_AT = 22 * KB
 ROUND_AT = 24 * KB
+ACT2_AT = 30 * KB
 GATES_AT = 26 * KB
 
 HOLDING_UNITS = (3, 7)
 SCALAR_UNIT = 6
+GPSIMD_UNITS = (3, 7)
 UNIT_BANKS = (0, 1, 2, 3, 4, 2, 3, 2)
 TURN_BANKS = (4, 3, 0, 1)
 SUM_BANKS = ((6, 7, 5, 4), (3, 0, 2, 1))
@@ -167,7 +170,10 @@ def tile_moe_wsel_b_silu_p_kernel(
                 stop=True,
             )
             if k not in acts:
-                acts[k] = keep.tile([P, H], F32, align_bytes=64, name="act%d" % k)
+                if k == 2:
+                    acts[k] = at(ACT2_AT, [P, H], F32, "act2")
+                else:
+                    acts[k] = keep.tile([P, H], F32, align_bytes=64, name="act%d" % k)
             words = slice(hidden.start // PACK, hidden.stop // PACK)
             nc.scalar.activation(
                 out=acts[k][:].rearrange("p (u m e) -> p u m e", u=2, e=2)[:, :, words, :],
@@ -176,13 +182,21 @@ def tile_moe_wsel_b_silu_p_kernel(
                 bias=biases[k][:, 0:1] if k in biases else 0.0,
             )
 
-        gated = [keep.tile([P, 2 * H], BF16, align_bytes=64, name="gated%d" % i) for i in range(4)]
+        gated = {}
 
         def apply_gate(k):
             half, r, cc = units[k]
             col = r * CHUNKS + 2 * half + cc
-            h_tok = gated[k // 2][:, cc * H:(cc + 1) * H]
-            if k == SCALAR_UNIT:
+            if k == 3:
+                gated[k] = at(ACT2_AT, [P, H], BF16, "gated3")
+            else:
+                gated[k] = keep.tile([P, H], BF16, align_bytes=64, name="gated%d" % k)
+            h_tok = gated[k][:]
+            if k in GPSIMD_UNITS:
+                nc.gpsimd.tensor_scalar(
+                    out=h_tok, in0=acts[k][:], scalar1=gate_cols[:, col:col + 1], scalar2=0.0, op0=MULT, op1=ADD
+                )
+            elif k == SCALAR_UNIT:
                 nc.scalar.activation(out=h_tok, in_=acts[k][:], func=COPY, scale=gate_cols[:, col:col + 1])
             else:
                 nc.vector.tensor_scalar(
@@ -191,10 +205,10 @@ def tile_moe_wsel_b_silu_p_kernel(
 
         def turn(i):
             turned = psum.tile([P, 2, 2, P], F32, tag="bank%d" % TURN_BANKS[i])
-            words = gated[i][:].bitcast(F32)
             for cc in range(2):
+                words = gated[2 * i + cc][:].bitcast(F32)
                 for u in range(2):
-                    nc.tensor.transpose(turned[:, cc, u, :], words[:, (2 * cc + u) * P:(2 * cc + u + 1) * P], ident[:])
+                    nc.tensor.transpose(turned[:, cc, u, :], words[:, u * P:(u + 1) * P], ident[:])
             grouped = keep.tile([P, 2 * P * PACK], BF16, align_bytes=64, name="h_grouped%d" % i)
             nc.scalar.copy(
                 out=grouped[:].bitcast(F32).rearrange("p (c t u) -> p c t u", c=2, u=2),

@@ -38,15 +38,16 @@ SCALES_AT = 15 * KB
 DEALT_AT = (18 * KB, 20 * KB)
 LAST_AT = 22 * KB
 ROUND_AT = 24 * KB
-ACT2_AT = 30 * KB
+ACT_AT = {3: 30 * KB}
+GATED_AT = {4: 30 * KB}
 GATES_AT = 26 * KB
 
-HOLDING_UNITS = (3, 7)
-SCALAR_UNIT = 6
-GPSIMD_UNITS = (3, 7)
+HOLDING_UNITS = ()
+SCALAR_UNIT = None
+GPSIMD_UNITS = (4, 5, 6)
 UNIT_BANKS = (0, 1, 2, 3, 4, 2, 3, 2)
 TURN_BANKS = (4, 3, 0, 1)
-SUM_BANKS = ((6, 7, 5, 4), (3, 0, 2, 1))
+SUM_BANKS = ((6, 7, 5, 4), (3, 2, 1, 0))
 VECTOR_ROUNDS = 160
 
 
@@ -170,8 +171,8 @@ def tile_moe_wsel_b_silu_p_kernel(
                 stop=True,
             )
             if k not in acts:
-                if k == 2:
-                    acts[k] = at(ACT2_AT, [P, H], F32, "act2")
+                if k in ACT_AT:
+                    acts[k] = at(ACT_AT[k], [P, H], F32, "act%d" % k)
                 else:
                     acts[k] = keep.tile([P, H], F32, align_bytes=64, name="act%d" % k)
             words = slice(hidden.start // PACK, hidden.stop // PACK)
@@ -187,8 +188,8 @@ def tile_moe_wsel_b_silu_p_kernel(
         def apply_gate(k):
             half, r, cc = units[k]
             col = r * CHUNKS + 2 * half + cc
-            if k == 3:
-                gated[k] = at(ACT2_AT, [P, H], BF16, "gated3")
+            if k in GATED_AT:
+                gated[k] = at(GATED_AT[k], [P, H], BF16, "gated%d" % k)
             else:
                 gated[k] = keep.tile([P, H], BF16, align_bytes=64, name="gated%d" % k)
             h_tok = gated[k][:]
@@ -203,18 +204,21 @@ def tile_moe_wsel_b_silu_p_kernel(
                     out=h_tok, in0=acts[k][:], scalar1=gate_cols[:, col:col + 1], scalar2=None, op0=MULT
                 )
 
-        def turn(i):
-            turned = psum.tile([P, 2, 2, P], F32, tag="bank%d" % TURN_BANKS[i])
-            for cc in range(2):
-                words = gated[2 * i + cc][:].bitcast(F32)
+        grouped = [keep.tile([P, 2 * P * PACK], BF16, align_bytes=64, name="h_grouped%d" % i) for i in range(4)]
+
+        def turn(ks, bank):
+            turned = psum.tile([P, len(ks), 2, P], F32, tag="bank%d" % bank)
+            for c, k in enumerate(ks):
+                words = gated[k][:].bitcast(F32)
                 for u in range(2):
-                    nc.tensor.transpose(turned[:, cc, u, :], words[:, u * P:(u + 1) * P], ident[:])
-            grouped = keep.tile([P, 2 * P * PACK], BF16, align_bytes=64, name="h_grouped%d" % i)
+                    nc.tensor.transpose(turned[:, c, u, :], words[:, u * P:(u + 1) * P], ident[:])
+            first = ks[0] % 2 * H
             nc.scalar.copy(
-                out=grouped[:].bitcast(F32).rearrange("p (c t u) -> p c t u", c=2, u=2),
+                out=grouped[ks[0] // 2][:, first:first + len(ks) * H].bitcast(F32).rearrange(
+                    "p (c t u) -> p c t u", c=len(ks), u=2
+                ),
                 in_=turned[:].rearrange("p c u t -> p c t u"),
             )
-            return grouped
 
         def quantize_hidden(i, grouped, codes):
             plane = keep.tile([P, HALF], U8, align_bytes=64, name="h_plane%d" % i)
@@ -240,7 +244,7 @@ def tile_moe_wsel_b_silu_p_kernel(
             )
 
         def pick_dealt(r):
-            dealt = at(DEALT_AT[r], [P, N], I32, "w2_codes%d" % r)
+            dealt = keep.tile([P, N], I32, align_bytes=64, name="w2_codes%d" % r)
             pick(w2_all[:].bitcast(U32), list2, r, dealt[:].bitcast(U32).rearrange("p (j m) -> p m j", j=PACK))
             return dealt
 
@@ -265,22 +269,22 @@ def tile_moe_wsel_b_silu_p_kernel(
         place_scale_rows(nc.sync, w2_plane, w2_plane, W2_ROWS)
         for k in range(2, 4):
             apply_gate(k)
-        w2_codes = [pick_dealt(0)]
+        w2_codes = [pick_dealt(r) for r in range(G)]
         for k in range(4, 6):
             apply_gate(k)
 
-        grouped = [turn(0)]
+        turn([0], 4)
         first_layer(7, UNIT_BANKS[7], whole)
+        turn([1], 0)
         apply_gate(6)
-        grouped.append(turn(1))
-        keep_clock(TURN_BANKS[0], H)
+        turn([2, 3], 3)
+        keep_clock(4, H)
         keep_clock(UNIT_BANKS[7], H // 2)
         h_codes = [keep.tile([P, HALF], I32, align_bytes=64, name="h_codes%d" % i) for i in range(4)]
         hq = [quantize_hidden(0, grouped[0], h_codes[0])]
         apply_gate(7)
-        w2_codes.append(pick_dealt(1))
-        for i in range(2, 4):
-            grouped.append(turn(i))
+        turn([4, 5], 1)
+        turn([6, 7], 0)
         for i in range(1, 4):
             hq.append(quantize_hidden(i, grouped[i], h_codes[i]))
 

@@ -82,7 +82,6 @@ def tile_moe_wsel_b_silu_p_kernel(
         for r, k in enumerate(HOLDING_UNITS):
             biases[k] = at(DEALT_AT[r], [P, 1], F32, "bias%d" % k)
 
-        nc.gpsimd.memset(w1_all[:, EARLY:EARLY + P], 0)
         nc.gpsimd.memset(zero_col[:, 0:1], 0.0)
         nc.gpsimd.memset(gate_rows[:], 0.0)
         gate_runs = gate.rearrange("r q (c p) -> (r q c) p", p=P)
@@ -97,13 +96,12 @@ def tile_moe_wsel_b_silu_p_kernel(
             pattern=[[-1, P]],
             channel_multiplier=1,
         )
-        for k in HOLDING_UNITS:
-            nc.gpsimd.memset(biases[k][:], 0.0)
-        nc.vector.tensor_copy(out=x_plane[:].bitcast(I32), in_=w1_all[:, EARLY:EARLY + P])
+        nc.gpsimd.memset(w2s_all[W2_ROWS + BLOCKS:P, :].bitcast(I32), 0)
+        nc.vector.memset(x_plane[:].bitcast(I32), 0)
+        nc.vector.memset(w1_all[:, EARLY:EARLY + 2], 0)
         nc.vector.memset(w1s_all[0:W1_ROWS, :].bitcast(I32), 0)
-        nc.vector.memset(w2s_all[0:W2_ROWS, :].bitcast(I32), 0)
-        nc.vector.memset(w2s_all[W2_ROWS + BLOCKS:P, :].bitcast(I32), 0)
         nc.vector.memset(w1_plane[:].bitcast(I32), 0)
+        nc.vector.memset(w2s_all[0:W2_ROWS, :].bitcast(I32), 0)
 
         nc.sync.dma_start(list1[:], offs)
         nc.sync.dma_start(out=w1s_all[W1_ROWS:W1_ROWS + BLOCKS, :].bitcast(I32), in_=w1_scales[0].bitcast(I32))

@@ -39,13 +39,14 @@ DEALT_AT = (18 * KB, 20 * KB)
 LAST_AT = 22 * KB
 ROUND_AT = 24 * KB
 ACT_AT = {3: 30 * KB}
-GATED_AT = {4: 30 * KB}
+GATED_AT = {4: 30 * KB, 6: W2_AT + 64}
 GATES_AT = 26 * KB
 
 HOLDING_UNITS = ()
 SCALAR_UNIT = None
-GPSIMD_UNITS = (4, 5, 6)
+GPSIMD_UNITS = (0, 4, 5)
 UNIT_BANKS = (0, 1, 2, 3, 4, 2, 3, 2)
+PART_BANKS = (6, 7, 5)
 TURN_BANKS = (4, 3, 0, 1)
 SUM_BANKS = ((6, 7, 5, 4), (3, 2, 1, 0))
 VECTOR_ROUNDS = 160
@@ -103,8 +104,8 @@ def tile_moe_wsel_b_silu_p_kernel(
         nc.vector.memset(w1_plane[:].bitcast(I32), 0)
         nc.vector.memset(w2s_all[0:W2_ROWS, :].bitcast(I32), 0)
 
-        nc.sync.dma_start(list1[:], offs)
         nc.sync.dma_start(out=w1s_all[W1_ROWS:W1_ROWS + BLOCKS, :].bitcast(I32), in_=w1_scales[0].bitcast(I32))
+        nc.sync.dma_start(list1[:], offs)
         nc.sync.dma_start(list2[:], offs2)
         nc.sync.dma_start(out=w2s_all[W2_ROWS:W2_ROWS + BLOCKS, :].bitcast(I32), in_=w2_scales[0].bitcast(I32))
         nc.sync.dma_start(out=w1_all[:, 0:EARLY], in_=words_of(w1_words)[:, 0:EARLY])
@@ -137,7 +138,7 @@ def tile_moe_wsel_b_silu_p_kernel(
         w1_codes = []
         for r in range(G):
             picked = keep.tile([P, H], I32, align_bytes=64, name="w1_codes%d" % r)
-            parts = 2 if r == 0 else 1
+            parts = 2
             for part in range(parts):
                 entries = slice((r * parts + part) * LIST_COLS // parts, (r * parts + part + 1) * LIST_COLS // parts)
                 nc.vector.tensor_copy(
@@ -251,16 +252,18 @@ def tile_moe_wsel_b_silu_p_kernel(
         gate_cols = at(GATES_AT, [P, G * CHUNKS], F32, "gate_cols")
         nc.scalar.copy(out=gate_cols[:], in_=gate_bank[:, 0:G * CHUNKS])
         whole = slice(0, H)
-        for part in range(2):
-            for k in range(2):
-                first_layer(k, (k + 6 * (1 - part)) % 8, slice(part * H // 2, (part + 1) * H // 2))
-        for k in range(2, 7):
+        for ks in (range(2), range(2, 3)):
+            for part in range(2):
+                for k in ks:
+                    bank = UNIT_BANKS[k] if part else PART_BANKS[k]
+                    first_layer(k, bank, slice(part * H // 2, (part + 1) * H // 2))
+        for k in range(3, 7):
             first_layer(k, UNIT_BANKS[k], whole)
 
-        w2s_second = at(SCALES_AT + 64, [P, N], U8, "w2s_second")
-        pick(w2s_all[:], list2, 1, w2s_second[:])
         w2_plane = at(SCALES_AT + 64 + N, [P, G * N], U8, "w2_plane")
         deal_scales(0, w2s_first)
+        w2s_second = at(SCALES_AT + 64, [P, N], U8, "w2s_second")
+        pick(w2s_all[:], list2, 1, w2s_second[:])
         for k in range(2):
             apply_gate(k)
         deal_scales(1, w2s_second)
@@ -279,8 +282,8 @@ def tile_moe_wsel_b_silu_p_kernel(
         keep_clock(4, H)
         keep_clock(UNIT_BANKS[7], H // 2)
         h_codes = [keep.tile([P, HALF], I32, align_bytes=64, name="h_codes%d" % i) for i in range(4)]
-        hq = [quantize_hidden(0, grouped[0], h_codes[0])]
         apply_gate(7)
+        hq = [quantize_hidden(0, grouped[0], h_codes[0])]
         turn([4, 5], 1)
         turn([6, 7], 0)
         for i in range(1, 4):

@@ -39,12 +39,12 @@ DEALT_AT = (18 * KB, 20 * KB)
 LAST_AT = 22 * KB
 ROUND_AT = 24 * KB
 ACT_AT = {3: 30 * KB}
-GATED_AT = {4: 30 * KB, 6: W2_AT + 64}
+GATED_AT = {4: 30 * KB}
 GATES_AT = 26 * KB
 
 HOLDING_UNITS = ()
 SCALAR_UNIT = None
-GPSIMD_UNITS = (0, 4, 5)
+GPSIMD_UNITS = (0, 4, 5, 6)
 UNIT_BANKS = (0, 1, 2, 3, 4, 2, 3, 2)
 PART_BANKS = (6, 7, 5)
 TURN_BANKS = (4, 3, 0, 1)
@@ -309,7 +309,7 @@ def tile_moe_wsel_b_silu_p_kernel(
             return sums
 
         def copy_out(half, sums, rows, j):
-            engine = nc.scalar.copy if j < 2 + half else nc.vector.tensor_copy
+            engine = nc.scalar.copy if j < 3 else nc.vector.tensor_copy
             engine(out=rows[:, j, :], in_=sums[j][:])
             first = j if half == 0 and j < 2 else j - 1
             if first == j or j % 2:

@@ -98,9 +98,9 @@ def tile_moe_wsel_b_silu_p_kernel(
             channel_multiplier=1,
         )
         nc.gpsimd.memset(w2s_all[W2_ROWS + BLOCKS:P, :].bitcast(I32), 0)
-        nc.vector.memset(x_plane[:].bitcast(I32), 0)
-        nc.vector.memset(w1_all[:, EARLY:EARLY + 2], 0)
+        nc.vector.memset(w1_all[:, EARLY:EARLY + P], 0)
         nc.vector.memset(w1s_all[0:W1_ROWS, :].bitcast(I32), 0)
+        nc.vector.tensor_copy(out=x_plane[:].bitcast(I32), in_=w1_all[:, EARLY:EARLY + P])
         nc.vector.memset(w1_plane[:].bitcast(I32), 0)
         nc.vector.memset(w2s_all[0:W2_ROWS, :].bitcast(I32), 0)
 

@@ -106,9 +106,9 @@ def tile_moe_wsel_b_silu_p_kernel(
 
         nc.sync.dma_start(out=w1s_all[W1_ROWS:W1_ROWS + BLOCKS, :].bitcast(I32), in_=w1_scales[0].bitcast(I32))
         nc.sync.dma_start(list1[:], offs)
-        nc.sync.dma_start(list2[:], offs2)
-        nc.sync.dma_start(out=w2s_all[W2_ROWS:W2_ROWS + BLOCKS, :].bitcast(I32), in_=w2_scales[0].bitcast(I32))
+        nc.scalar.dma_start(out=w2s_all[W2_ROWS:W2_ROWS + BLOCKS, :].bitcast(I32), in_=w2_scales[0].bitcast(I32))
         nc.sync.dma_start(out=w1_all[:, 0:EARLY], in_=words_of(w1_words)[:, 0:EARLY])
+        nc.sync.dma_start(list2[:], offs2)
         for i in range(PACK):
             nc.sync.dma_start(out=x_plane[X_ROW + i:P:32, :].bitcast(I32), in_=x_scales[0, i:BLOCKS:4, :].bitcast(I32))
         nc.sync.dma_start(out=w1_all[:, EARLY:E * H], in_=words_of(w1_words)[:, EARLY:E * H])

@@ -104,9 +104,9 @@ def tile_moe_wsel_b_silu_p_kernel(
         nc.vector.memset(w1_plane[:].bitcast(I32), 0)
         nc.vector.memset(w2s_all[0:W2_ROWS, :].bitcast(I32), 0)
 
-        nc.sync.dma_start(out=w1s_all[W1_ROWS:W1_ROWS + BLOCKS, :].bitcast(I32), in_=w1_scales[0].bitcast(I32))
+        nc.scalar.dma_start(out=w1s_all[W1_ROWS:W1_ROWS + BLOCKS, :].bitcast(I32), in_=w1_scales[0].bitcast(I32))
         nc.sync.dma_start(list1[:], offs)
-        nc.scalar.dma_start(out=w2s_all[W2_ROWS:W2_ROWS + BLOCKS, :].bitcast(I32), in_=w2_scales[0].bitcast(I32))
+        nc.sync.dma_start(out=w2s_all[W2_ROWS:W2_ROWS + BLOCKS, :].bitcast(I32), in_=w2_scales[0].bitcast(I32))
         nc.sync.dma_start(out=w1_all[:, 0:EARLY], in_=words_of(w1_words)[:, 0:EARLY])
         nc.sync.dma_start(list2[:], offs2)
         for i in range(PACK):

@@ -133,8 +133,8 @@ def tile_moe_wsel_b_silu_p_kernel(
         nc.sync.dma_start(out=x_codes[1][:], in_=words_of(x_words)[:, HALF:T])
         w2_all = at(W2_AT, [P, E * N], I32, "w2_all")
         nc.sync.dma_start(out=w2_all[:], in_=words_of(w2_words))
-        w2s_first = keep.tile([P, N], U8, align_bytes=64)
-        pick(w2s_all[:], list2, 0, w2s_first[:])
+        w2s_picked = keep.tile([P, G * N], U8, align_bytes=64)
+        nc.vector.tensor_copy(out=w2s_picked[:], in_=w2s_all[:].indirect(list2[:]))
         w1_codes = []
         for r in range(G):
             picked = keep.tile([P, H], I32, align_bytes=64, name="w1_codes%d" % r)
@@ -227,7 +227,7 @@ def tile_moe_wsel_b_silu_p_kernel(
         def deal_scales(r, picked):
             nc.vector.tensor_copy(
                 out=w2_plane[:, r * N:(r + 1) * N].rearrange("p (j b i) -> p b j i", j=PACK, i=16),
-                in_=picked[:].rearrange("p (b i j) -> p b j i", j=PACK, i=16),
+                in_=picked.rearrange("p (b i j) -> p b j i", j=PACK, i=16),
             )
 
         def keep_clock(bank, width):
@@ -261,12 +261,10 @@ def tile_moe_wsel_b_silu_p_kernel(
             first_layer(k, UNIT_BANKS[k], whole)
 
         w2_plane = at(SCALES_AT + 64 + N, [P, G * N], U8, "w2_plane")
-        deal_scales(0, w2s_first)
-        w2s_second = at(SCALES_AT + 64, [P, N], U8, "w2s_second")
-        pick(w2s_all[:], list2, 1, w2s_second[:])
+        deal_scales(0, w2s_picked[:, 0:N])
         for k in range(2):
             apply_gate(k)
-        deal_scales(1, w2s_second)
+        deal_scales(1, w2s_picked[:, N:G * N])
         place_scale_rows(nc.sync, w2_plane, w2_plane, W2_ROWS)
         for k in range(2, 4):
             apply_gate(k)

@@ -38,13 +38,13 @@ SCALES_AT = 15 * KB
 DEALT_AT = (18 * KB, 20 * KB)
 LAST_AT = 22 * KB
 ROUND_AT = 24 * KB
-ACT_AT = {3: 30 * KB}
-GATED_AT = {4: 30 * KB}
+ACT_AT = {}
+GATED_AT = {6: W2_AT + KB, 7: W2_AT + 2 * KB}
 GATES_AT = 26 * KB
 
 HOLDING_UNITS = ()
 SCALAR_UNIT = None
-GPSIMD_UNITS = (0, 4, 5, 6)
+GPSIMD_UNITS = (3, 4, 5)
 UNIT_BANKS = (0, 1, 2, 3, 4, 2, 3, 2)
 PART_BANKS = (6, 7, 5)
 TURN_BANKS = (4, 3, 0, 1)

@@ -29,7 +29,7 @@ KB = 1024
 X_ROW = 8
 W1_ROWS = 112
 W2_ROWS = 48
-EARLY = 2048
+EARLY = 1536
 
 W1S_AT = 0
 X_LATE_AT = 2 * KB - 64

@@ -44,7 +44,7 @@ GATES_AT = 26 * KB
 
 HOLDING_UNITS = ()
 SCALAR_UNIT = None
-GPSIMD_UNITS = (3, 4, 5)
+GPSIMD_UNITS = (4, 5)
 UNIT_BANKS = (0, 1, 2, 3, 4, 2, 3, 2)
 PART_BANKS = (6, 7, 5)
 TURN_BANKS = (4, 3, 0, 1)

from contextlib import ExitStack

import concourse.mybir as mybir

K, T, E, G, H, N = 512, 512, 6, 2, 512, 512
FLOPS = 2 * G * T * (K * H + H * N)

F32 = mybir.dt.float32
BF16 = mybir.dt.bfloat16
I32 = mybir.dt.int32
U32 = mybir.dt.uint32
U16 = mybir.dt.uint16
U8 = mybir.dt.uint8
FP8X4 = mybir.dt.float8_e4m3fn_x4
SILU = mybir.ActivationFunctionType.Silu
COPY = mybir.ActivationFunctionType.Copy
MULT = mybir.AluOpType.mult
ADD = mybir.AluOpType.add

P = 128
PACK = 4
QUADRANTS = 4
BLOCKS = 16
CHUNKS = T // P
HALF = T // 2
LIST_COLS = H // 16
KB = 1024

X_ROW = 8
W1_ROWS = 112
W2_ROWS = 48
EARLY = 1536

W1S_AT = 0
X_LATE_AT = 2 * KB - 64
W2_AT = 3 * KB - 64
SCALES_AT = 15 * KB
DEALT_AT = (18 * KB, 20 * KB)
LAST_AT = 22 * KB
ROUND_AT = 24 * KB
ACT_AT = {}
GATED_AT = {6: W2_AT + KB, 7: W2_AT + 2 * KB}
GATES_AT = 26 * KB

HOLDING_UNITS = ()
SCALAR_UNIT = None
GPSIMD_UNITS = (4, 5)
UNIT_BANKS = (0, 1, 2, 3, 4, 2, 3, 2)
PART_BANKS = (6, 7, 5)
TURN_BANKS = (4, 3, 0, 1)
SUM_BANKS = ((6, 7, 5, 4), (3, 2, 1, 0))
VECTOR_ROUNDS = 160


def words_of(packed):
    return packed[0].rearrange("p m d -> p (m d)").bitcast(I32)


def tile_moe_wsel_b_silu_p_kernel(
    tc, x_words, x_scales, w1_words, w1_scales, w2_words, w2_scales, gate, offs, offs2, out_0, out_1, out_2
):
    nc = tc.nc
    with ExitStack() as ctx:
        keep = ctx.enter_context(tc.tile_pool(name="keep", bufs=1))
        placed = ctx.enter_context(tc.tile_pool(name="placed", bufs=1))
        psum = ctx.enter_context(tc.psum_pool(name="psum", bufs=1))

        def at(offset, shape, dtype, name):
            return placed.tile(shape, dtype, align_bytes=64, offset=offset, name=name)

        list1 = keep.tile([P, G * LIST_COLS], U16)
        list2 = keep.tile([P, G * LIST_COLS], U16)
        w1s_all = at(W1S_AT, [P, E * H], U8, "w1s_all")
        w2s_all = keep.tile([P, E * N], U8, align_bytes=64)
        x_plane = keep.tile([P, T], U8, align_bytes=64)
        w1_plane = keep.tile([P, G * H], U8, align_bytes=64)
        w1_all = keep.tile([P, E * H], I32, align_bytes=64)
        zeros = keep.tile([P, P], F32, align_bytes=64)
        gate_rows = keep.tile([P, P], F32, align_bytes=64)
        ident = keep.tile([P, P], F32)
        zero_col = at(GATES_AT, [P, 32], F32, "zero_col")
        biases = {0: keep.tile([P, 1], F32, align_bytes=64, name="bias0")}
        for r, k in enumerate(HOLDING_UNITS):
            biases[k] = at(DEALT_AT[r], [P, 1], F32, "bias%d" % k)

        nc.gpsimd.memset(zero_col[:, 0:1], 0.0)
        nc.gpsimd.memset(gate_rows[:], 0.0)
        gate_runs = gate.rearrange("r q (c p) -> (r q c) p", p=P)
        nc.gpsimd.dma_start(out=gate_rows[0:G * CHUNKS, :], in_=gate_runs[0:G * P * CHUNKS:P + 1, :])
        nc.gpsimd.memset(zeros[:], 0.0)
        nc.gpsimd.affine_select(
            out=ident[:],
            in_=zeros[:],
            compare_op=mybir.AluOpType.not_equal,
            fill=1.0,
            base=0,
            pattern=[[-1, P]],
            channel_multiplier=1,
        )
        nc.gpsimd.memset(w2s_all[W2_ROWS + BLOCKS:P, :].bitcast(I32), 0)
        nc.vector.memset(w1_all[:, EARLY:EARLY + P], 0)
        nc.vector.memset(w1s_all[0:W1_ROWS, :].bitcast(I32), 0)
        nc.vector.tensor_copy(out=x_plane[:].bitcast(I32), in_=w1_all[:, EARLY:EARLY + P])
        nc.vector.memset(w1_plane[:].bitcast(I32), 0)
        nc.vector.memset(w2s_all[0:W2_ROWS, :].bitcast(I32), 0)

        nc.scalar.dma_start(out=w1s_all[W1_ROWS:W1_ROWS + BLOCKS, :].bitcast(I32), in_=w1_scales[0].bitcast(I32))
        nc.sync.dma_start(list1[:], offs)
        nc.sync.dma_start(out=w2s_all[W2_ROWS:W2_ROWS + BLOCKS, :].bitcast(I32), in_=w2_scales[0].bitcast(I32))
        nc.sync.dma_start(out=w1_all[:, 0:EARLY], in_=words_of(w1_words)[:, 0:EARLY])
        nc.sync.dma_start(list2[:], offs2)
        for i in range(PACK):
            nc.sync.dma_start(out=x_plane[X_ROW + i:P:32, :].bitcast(I32), in_=x_scales[0, i:BLOCKS:4, :].bitcast(I32))
        nc.sync.dma_start(out=w1_all[:, EARLY:E * H], in_=words_of(w1_words)[:, EARLY:E * H])
        x_codes = [at(GATES_AT + 64, [P, HALF], I32, "x_early")]
        nc.sync.dma_start(out=x_codes[0][:], in_=words_of(x_words)[:, 0:HALF])
        nc.scalar.activation(out=biases[0][:, 0:1], in_=zero_col[:, 0:1], func=SILU)

        def place_scale_rows(queue, plane, rows, first_row):
            for q in range(QUADRANTS):
                queue.dma_start(
                    out=plane[32 * q:32 * q + 4, :].bitcast(I32),
                    in_=rows[first_row + 4 * q:first_row + 4 * q + 4, :].bitcast(I32),
                )

        def pick(window, offsets, r, out):
            nc.vector.tensor_copy(out=out, in_=window.indirect(offsets[:, r * LIST_COLS:(r + 1) * LIST_COLS]))

        w1s_picked = at(SCALES_AT, [P, G * H], U8, "w1s_picked")
        nc.vector.tensor_copy(out=w1s_picked[:], in_=w1s_all[:].indirect(list1[:]))
        place_scale_rows(nc.sync, w1_plane, w1s_picked, W1_ROWS)
        x_codes.append(at(X_LATE_AT, [P, HALF], I32, "x_late"))
        nc.sync.dma_start(out=x_codes[1][:], in_=words_of(x_words)[:, HALF:T])
        w2_all = at(W2_AT, [P, E * N], I32, "w2_all")
        nc.sync.dma_start(out=w2_all[:], in_=words_of(w2_words))
        w2s_picked = keep.tile([P, G * N], U8, align_bytes=64)
        nc.vector.tensor_copy(out=w2s_picked[:], in_=w2s_all[:].indirect(list2[:]))
        w1_codes = []
        for r in range(G):
            picked = keep.tile([P, H], I32, align_bytes=64, name="w1_codes%d" % r)
            parts = 2
            for part in range(parts):
                entries = slice((r * parts + part) * LIST_COLS // parts, (r * parts + part + 1) * LIST_COLS // parts)
                nc.vector.tensor_copy(
                    out=picked[:, part * H // parts:(part + 1) * H // parts].bitcast(U32),
                    in_=w1_all[:].bitcast(U32).indirect(list1[:, entries]),
                )
            w1_codes.append(picked)

        y_codes = keep.tile([P, T], I32, align_bytes=64)
        y_plane = keep.tile([P, T], U8, align_bytes=64)
        out_rows = out_0.rearrange("(p j) t -> p j t", j=PACK)
        out_words = words_of(out_1)

        units = [(half, r, cc) for half in range(2) for r in range(G) for cc in range(2)]
        acts = {}

        def first_layer(k, bank, hidden):
            half, r, cc = units[k]
            tokens = slice((2 * half + cc) * P, (2 * half + cc + 1) * P)
            width = hidden.stop - hidden.start
            pre = psum.tile([P, H], F32, tag="bank%d" % bank)
            nc.tensor.matmul_mx(
                out=pre[:, 0:width],
                lhsT=x_codes[half][:, cc * P:(cc + 1) * P].bitcast(FP8X4),
                lhsT_scale=x_plane[X_ROW:P, tokens],
                rhs=w1_codes[r][:, hidden].bitcast(FP8X4),
                rhs_scale=w1_plane[:, r * H + hidden.start:r * H + hidden.stop],
                start=True,
                stop=True,
            )
            if k not in acts:
                if k in ACT_AT:
                    acts[k] = at(ACT_AT[k], [P, H], F32, "act%d" % k)
                else:
                    acts[k] = keep.tile([P, H], F32, align_bytes=64, name="act%d" % k)
            words = slice(hidden.start // PACK, hidden.stop // PACK)
            nc.scalar.activation(
                out=acts[k][:].rearrange("p (u m e) -> p u m e", u=2, e=2)[:, :, words, :],
                in_=pre[:, 0:width].rearrange("p (m u e) -> p u m e", u=2, e=2),
                func=SILU,
                bias=biases[k][:, 0:1] if k in biases else 0.0,
            )

        gated = {}

        def apply_gate(k):
            half, r, cc = units[k]
            col = r * CHUNKS + 2 * half + cc
            if k in GATED_AT:
                gated[k] = at(GATED_AT[k], [P, H], BF16, "gated%d" % k)
            else:
                gated[k] = keep.tile([P, H], BF16, align_bytes=64, name="gated%d" % k)
            h_tok = gated[k][:]
            if k in GPSIMD_UNITS:
                nc.gpsimd.tensor_scalar(
                    out=h_tok, in0=acts[k][:], scalar1=gate_cols[:, col:col + 1], scalar2=0.0, op0=MULT, op1=ADD
                )
            elif k == SCALAR_UNIT:
                nc.scalar.activation(out=h_tok, in_=acts[k][:], func=COPY, scale=gate_cols[:, col:col + 1])
            else:
                nc.vector.tensor_scalar(
                    out=h_tok, in0=acts[k][:], scalar1=gate_cols[:, col:col + 1], scalar2=None, op0=MULT
                )

        grouped = [keep.tile([P, 2 * P * PACK], BF16, align_bytes=64, name="h_grouped%d" % i) for i in range(4)]

        def turn(ks, bank):
            turned = psum.tile([P, len(ks), 2, P], F32, tag="bank%d" % bank)
            for c, k in enumerate(ks):
                words = gated[k][:].bitcast(F32)
                for u in range(2):
                    nc.tensor.transpose(turned[:, c, u, :], words[:, u * P:(u + 1) * P], ident[:])
            first = ks[0] % 2 * H
            nc.scalar.copy(
                out=grouped[ks[0] // 2][:, first:first + len(ks) * H].bitcast(F32).rearrange(
                    "p (c t u) -> p c t u", c=len(ks), u=2
                ),
                in_=turned[:].rearrange("p c u t -> p c t u"),
            )

        def quantize_hidden(i, grouped, codes):
            plane = keep.tile([P, HALF], U8, align_bytes=64, name="h_plane%d" % i)
            nc.vector.quantize_mx(out=codes[:].bitcast(FP8X4), scales=plane[:], in_=grouped[:])
            return codes, plane

        def deal_scales(r, picked):
            nc.vector.tensor_copy(
                out=w2_plane[:, r * N:(r + 1) * N].rearrange("p (j b i) -> p b j i", j=PACK, i=16),
                in_=picked.rearrange("p (b i j) -> p b j i", j=PACK, i=16),
            )

        def keep_clock(bank, width):
            unread = psum.tile([P, width], F32, tag="bank%d" % bank, name="unread%d" % bank)
            nc.tensor.matmul_mx(
                out=unread[:],
                lhsT=x_codes[0][:, 0:P].bitcast(FP8X4),
                lhsT_scale=x_plane[X_ROW:P, 0:P],
                rhs=w1_codes[0][:, 0:width].bitcast(FP8X4),
                rhs_scale=w1_plane[:, 0:width],
                start=True,
                stop=True,
            )

        def pick_dealt(r):
            dealt = keep.tile([P, N], I32, align_bytes=64, name="w2_codes%d" % r)
            pick(w2_all[:].bitcast(U32), list2, r, dealt[:].bitcast(U32).rearrange("p (j m) -> p m j", j=PACK))
            return dealt

        gate_bank = psum.tile([P, P], F32, tag="bank5")
        nc.tensor.transpose(gate_bank[:], gate_rows[:], ident[:])
        gate_cols = at(GATES_AT, [P, G * CHUNKS], F32, "gate_cols")
        nc.scalar.copy(out=gate_cols[:], in_=gate_bank[:, 0:G * CHUNKS])
        whole = slice(0, H)
        for ks in (range(2), range(2, 3)):
            for part in range(2):
                for k in ks:
                    bank = UNIT_BANKS[k] if part else PART_BANKS[k]
                    first_layer(k, bank, slice(part * H // 2, (part + 1) * H // 2))
        for k in range(3, 7):
            first_layer(k, UNIT_BANKS[k], whole)

        w2_plane = at(SCALES_AT + 64 + N, [P, G * N], U8, "w2_plane")
        deal_scales(0, w2s_picked[:, 0:N])
        for k in range(2):
            apply_gate(k)
        deal_scales(1, w2s_picked[:, N:G * N])
        place_scale_rows(nc.sync, w2_plane, w2_plane, W2_ROWS)
        for k in range(2, 4):
            apply_gate(k)
        w2_codes = [pick_dealt(r) for r in range(G)]
        for k in range(4, 6):
            apply_gate(k)

        turn([0], 4)
        first_layer(7, UNIT_BANKS[7], whole)
        turn([1], 0)
        apply_gate(6)
        turn([2, 3], 3)
        keep_clock(4, H)
        keep_clock(UNIT_BANKS[7], H // 2)
        h_codes = [keep.tile([P, HALF], I32, align_bytes=64, name="h_codes%d" % i) for i in range(4)]
        apply_gate(7)
        hq = [quantize_hidden(0, grouped[0], h_codes[0])]
        turn([4, 5], 1)
        turn([6, 7], 0)
        for i in range(1, 4):
            hq.append(quantize_hidden(i, grouped[i], h_codes[i]))

        def second_layer(half):
            sums = [
                psum.tile([P, HALF], F32, tag="bank%d" % SUM_BANKS[half][j], name="sums%d%d" % (half, j))
                for j in range(PACK)
            ]
            for r in range(G):
                codes, plane = hq[G * half + r]
                for j in range(PACK):
                    nc.tensor.matmul_mx(
                        out=sums[j][:],
                        lhsT=w2_codes[r][:, j * P:(j + 1) * P].bitcast(FP8X4),
                        lhsT_scale=w2_plane[:, r * N + j * P:r * N + (j + 1) * P],
                        rhs=codes[:].bitcast(FP8X4),
                        rhs_scale=plane[:],
                        start=(r == 0),
                        stop=(r == G - 1),
                    )
            return sums

        def copy_out(half, sums, rows, j):
            engine = nc.scalar.copy if j < 3 else nc.vector.tensor_copy
            engine(out=rows[:, j, :], in_=sums[j][:])
            first = j if half == 0 and j < 2 else j - 1
            if first == j or j % 2:
                nc.sync.dma_start(
                    out=out_rows[:, first:j + 1, half * HALF:(half + 1) * HALF], in_=rows[:, first:j + 1, :]
                )

        def round_and_group(engine, y_rows, out):
            engine(
                out=out.rearrange("p (b i j) -> p b j i", j=PACK, i=4),
                in_=y_rows.rearrange("p j (b i) -> p b j i", i=4),
            )

        def quantize_result(half, values):
            tokens = slice(half * HALF, (half + 1) * HALF)
            nc.vector.quantize_mx(out=y_codes[:, tokens].bitcast(FP8X4), scales=y_plane[:, tokens], in_=values[:])
            nc.sync.dma_start(out=out_words[:, tokens], in_=y_codes[:, tokens])

        sums = [second_layer(half) for half in range(2)]
        y = [keep.tile([P, PACK, HALF], F32, align_bytes=64, name="y%d" % half) for half in range(2)]
        rounded = [keep.tile([P, PACK * HALF], BF16, align_bytes=64, name="rounded%d" % half) for half in range(2)]
        for j in range(PACK):
            copy_out(0, sums[0], y[0], j)
        round_and_group(nc.vector.tensor_copy, y[0][:], rounded[0][:])
        for j in range(PACK):
            copy_out(1, sums[1], y[1], j)
        quantize_result(0, rounded[0])
        round_and_group(nc.vector.tensor_copy, y[1][:, :, 0:VECTOR_ROUNDS], rounded[1][:, 0:PACK * VECTOR_ROUNDS])
        round_and_group(nc.scalar.copy, y[1][:, :, VECTOR_ROUNDS:HALF], rounded[1][:, PACK * VECTOR_ROUNDS:PACK * HALF])
        quantize_result(1, rounded[1])

        for i in range(PACK):
            queue = nc.scalar if i % 2 else nc.sync
            queue.dma_start(out=out_2[0, i:BLOCKS:4, :].bitcast(I32), in_=y_plane[i:P:32, :].bitcast(I32))
